import numpy as np
import ml_dtypes


def mxq(x, axis, fmt="e4m3"):
    dtype, down = {"e4m3": (ml_dtypes.float8_e4m3fn, 7), "e5m2": (ml_dtypes.float8_e5m2, 14)}[fmt]
    v = np.moveaxis(np.asarray(x, np.float32).astype(ml_dtypes.bfloat16).astype(np.float64), axis, -1)
    blocks = v.reshape(v.shape[:-1] + (-1, 32))
    amax = np.abs(blocks).max(-1, keepdims=True)
    byte = np.maximum(np.where(amax > 0, np.frexp(amax)[1] - 1 + 127, 0) - down, 1)
    scale = np.exp2(byte - 127.0)
    codes = (blocks / scale).astype(np.float32).astype(dtype).astype(np.float64)
    return np.moveaxis((codes * scale).reshape(v.shape), -1, axis)


WIDE = False


def mx_kscale(k):
    if not WIDE:
        return np.ones(k)
    levels = np.array([10, -10, 5, -5, 0])
    if k % 512:
        return np.exp2(np.random.permutation(np.resize(levels, k // 32))).repeat(32)
    a = np.empty((k // 512, 16))
    for p in range(k // 512):
        a[p, :8] = np.random.permutation(np.resize(levels, 8))
        for g in range(8):
            far = levels[np.abs(levels - a[p, g]) >= 10]
            a[p, g + 8] = far[np.random.randint(len(far))]
    return np.exp2(a.ravel()).repeat(32)


def f64(x):
    return np.asarray(x).astype(np.float64)


def striped(idx):
    return np.tile(np.asarray(idx).reshape(-1, 16).T, (8, 1)).astype(np.uint16)


def unstriped(offs):
    return offs[:16].T.reshape(-1).astype(np.int64)


E2M1 = np.array([0.0, 0.5, 1.0, 1.5, 2.0, 3.0, 4.0, 6.0, -0.0, -0.5, -1.0, -1.5, -2.0, -3.0, -4.0, -6.0])


def pack_weight(w, fmt):
    k, n = w.shape
    w = f64(np.asarray(w, np.float32).astype(ml_dtypes.bfloat16)).reshape(k // 32, 32, n)
    amax = np.abs(w).max(1)
    if fmt == "e4m3":
        byte = np.frexp(amax)[1] - 1 + 127 - 7
    else:
        mant, ex = np.frexp(amax / 6.0)
        byte = np.where(mant > 0.5, ex, ex - 1) + 127
    byte = np.clip(np.where(amax > 0, byte, 1), 1, 254)
    scaled = (w * np.exp2(127.0 - byte)[:, None, :]).reshape(k, n).astype(np.float32)
    by_word = np.ascontiguousarray(scaled.reshape(k // 512, 128, 4, n).transpose(0, 1, 3, 2))
    if fmt == "e4m3":
        words = by_word.astype(ml_dtypes.float8_e4m3fn).view(np.uint8)
    else:
        c = by_word.astype(ml_dtypes.float4_e2m1fn).view(np.uint8) & 0xF
        words = (c[..., 0::2] | (c[..., 1::2] << 4)).reshape(k // 512, 128, 2 * n)
    return np.ascontiguousarray(words), np.ascontiguousarray(byte.astype(np.uint8).reshape(k // 512, 16, n))


def unpack_weight(words, scales, fmt):
    g, _, n = scales.shape
    words = np.ascontiguousarray(words).reshape(g, 128, n, -1)
    if fmt == "e4m3":
        vals = words.view(ml_dtypes.float8_e4m3fn).astype(np.float64)
    else:
        nib = np.empty((g, 128, n, 4), np.uint8)
        nib[..., 0::2] = words & 0xF
        nib[..., 1::2] = words >> 4
        vals = E2M1[nib]
    vals = vals * np.repeat(np.exp2(scales.astype(np.float64) - 127.0), 8, axis=1)[..., None]
    return vals.transpose(0, 1, 3, 2).reshape(g * 512, n)


def sigmoid(v):
    return 1.0 / (1.0 + np.exp(-v))


B, N, T, D, NQ = 1, 512, 2048, 512, 256


def setup_inputs():
    n = np.random.standard_normal
    idx = np.random.permutation(T)[:B * N]
    s = mx_kscale(D)[:, None]
    kp = pack_weight(n((D, T)) / s, "e4m3")
    return {
        "qT": (n((B, D, NQ)) * s * (1.00 / np.sqrt(D))).astype(np.float32),
        "k_words": kp[0],
        "k_scales": kp[1],
        "kb": np.tile(n(2048), (128, 1)).astype(np.float32),
        "th": (n((B, NQ, 1))).astype(np.float32),
        "offs": striped(idx),
    }


def reference(qT, k_words, k_scales, kb, th, offs):
    idx = unstriped(offs)
    pick = lambda x, which: x[:, which].reshape(x.shape[0], B, -1).transpose(1, 0, 2)
    k = unpack_weight(k_words, k_scales, "e4m3")
    kg = pick(k, idx)
    qq = mxq(f64(qT), 1, "e4m3")
    a = qq.transpose(0, 2, 1) @ kg
    y = sigmoid(a + pick(f64(kb), idx)[:, :1, :] - f64(th))
    out = np.zeros((B, NQ, T))
    for b in range(B):
        out[b][:, idx[b * N:(b + 1) * N]] = y[b]
    return out

@@ -1,0 +1,150 @@
+from contextlib import ExitStack
+
+import concourse.mybir as mybir
+from concourse.masks import make_identity
+
+F32 = mybir.dt.float32
+BF16 = mybir.dt.bfloat16
+I32 = mybir.dt.int32
+U32 = mybir.dt.uint32
+U16 = mybir.dt.uint16
+U8 = mybir.dt.uint8
+FP8X4 = mybir.dt.float8_e4m3fn_x4
+ACT = mybir.ActivationFunctionType
+ALU = mybir.AluOpType
+
+P = 128
+PACK = 4
+T = 2048
+N = 512
+NQ = 256
+D = 512
+HALF = N // 2
+CHUNKS = N // P
+KB_ROW = P - 1
+ZERO_PIECE = 512
+
+FLOPS = 2 * NQ * N * D
+BYTES = 4 * D * NQ + D * T + 16 * T + 4 * T + 4 * NQ + 2 * P * (N // 16) + 4 * NQ * T
+
+
+def tile_attend_sigscat_topk_kernel(tc, qT, k_words, k_scales, kb, th, offs, out):
+    nc = tc.nc
+    with ExitStack() as ctx:
+        sb = ctx.enter_context(tc.tile_pool(name="sb", bufs=1))
+        ps = ctx.enter_context(tc.psum_pool(name="ps", bufs=1))
+
+        offsets = sb.tile([P, N // 16], U16, name="offsets")
+        nc.sync.dma_start(offsets[:], offs)
+        half_offsets = [offsets[:, u * (HALF // 16) : (u + 1) * (HALF // 16)] for u in range(2)]
+
+        scale_pool = sb.tile([P, T // 4], I32, name="scale_pool")
+        nc.vector.memset(scale_pool[:], 0)
+        kb_pool = sb.tile([P, T], F32, name="kb_pool", tag="wide0")
+        nc.vector.memset(kb_pool[0:KB_ROW, :], 0.0)
+        nc.sync.dma_start(kb_pool[KB_ROW:P, :], kb[0:1, :])
+
+        q_raw = sb.tile([P, PACK, NQ], F32, name="q_raw", tag="wide1")
+        nc.sync.dma_start(q_raw[:], qT[0].rearrange("(p j) w -> p j w", j=PACK))
+        for quad in range(4):
+            nc.sync.dma_start(
+                scale_pool[32 * quad : 32 * quad + 4, :], k_scales[0, 4 * quad : 4 * quad + 4, :].bitcast(I32)
+            )
+        word_pool = sb.tile([P, T], I32, name="word_pool")
+        nc.sync.dma_start(word_pool[:], k_words[0].rearrange("p t r -> p (t r)").bitcast(I32))
+        th_sb = sb.tile([P, 2], F32, name="th_sb")
+        with nc.allow_non_contiguous_dma(reason="one threshold a partition for each of the two query tiles"):
+            nc.sync.dma_start(th_sb[:], th[0, :, 0].rearrange("(h p) -> p h", p=P))
+
+        ident = sb.tile([P, P], F32, name="ident")
+        make_identity(nc, ident[:])
+        warm = sb.tile([P, 1], F32, name="warm")
+        nc.scalar.activation(warm[:], ident[:, 0:1], ACT.Sigmoid)
+
+        kb_listed = sb.tile([P, N], F32, name="kb_listed")
+        nc.vector.tensor_copy(kb_listed[:], kb_pool[:].indirect(offsets[:]))
+        k_scale = sb.tile([P, N], U8, name="k_scale", align_bytes=64)
+        nc.vector.tensor_copy(k_scale[:], scale_pool[:].bitcast(U8).indirect(offsets[:]))
+
+        kb_turned = ps.tile([P, CHUNKS, P], F32, name="kb_turned")
+        for c in range(CHUNKS):
+            nc.tensor.transpose(kb_turned[:, c, :], kb_listed[:, c * P : (c + 1) * P], ident[:])
+        kb_col = sb.tile([P, CHUNKS], F32, name="kb_col")
+        nc.scalar.copy(kb_col[:], kb_turned[:, :, KB_ROW])
+        kb_spread = ps.tile([P, CHUNKS, P], F32, name="kb_spread")
+        for c in range(CHUNKS):
+            nc.tensor.transpose(kb_spread[:, c, :], kb_col[:, c : c + 1].to_broadcast([P, P]), ident[:])
+
+        q_bf = sb.tile([P, NQ, PACK], BF16, name="q_bf", align_bytes=64)
+        q_code = sb.tile([P, NQ], U32, name="q_code", align_bytes=64)
+        q_scale = sb.tile([P, NQ], U8, name="q_scale", align_bytes=64)
+        for h in range(2):
+            rows = slice(h * P, (h + 1) * P)
+            nc.scalar.copy(q_bf[:, rows, :], q_raw[:, :, rows].rearrange("p j w -> p w j"))
+        for h in range(2):
+            rows = slice(h * P, (h + 1) * P)
+            nc.vector.quantize_mx(
+                out=q_code[:, rows].bitcast(FP8X4),
+                scales=q_scale[:, rows],
+                in_=q_bf[:, rows, :].rearrange("p w j -> p (w j)"),
+            )
+
+        kb_rows = sb.tile([P, N], F32, name="kb_rows")
+        nc.scalar.copy(kb_rows[:], kb_spread[:].rearrange("p c n -> p (c n)"))
+
+        maps = [sb.tile([P, T], F32, name="map%d" % h, tag="wide%d" % h) for h in range(2)]
+        for h in range(2):
+            for c0 in range(0, T, ZERO_PIECE):
+                nc.gpsimd.memset(maps[h][:, c0 : c0 + ZERO_PIECE], 0.0)
+
+        k_code = sb.tile([P, N], U32, name="k_code", align_bytes=64)
+        for u in range(2):
+            cols = slice(u * HALF, (u + 1) * HALF)
+            nc.vector.tensor_copy(k_code[:, cols], word_pool[:].bitcast(U32).indirect(half_offsets[u]))
+
+        neg_th = sb.tile([P, 2], F32, name="neg_th")
+        nc.scalar.mul(neg_th[:], th_sb[:], -1.0)
+
+        z0 = sb.tile([P, N], F32, name="z0")
+        y0 = sb.tile([P, N], F32, name="y0")
+        for u in range(2):
+            cols = slice(u * HALF, (u + 1) * HALF)
+            a0 = ps.tile([P, HALF], F32, name="a0_%d" % u)
+            nc.tensor.matmul_mx(
+                out=a0[:],
+                lhsT=q_code[:, 0:P].bitcast(FP8X4),
+                lhsT_scale=q_scale[:, 0:P],
+                rhs=k_code[:, cols].bitcast(FP8X4),
+                rhs_scale=k_scale[:, cols],
+                start=True,
+                stop=True,
+            )
+            nc.vector.tensor_tensor(z0[:, cols], a0[:], kb_rows[:, cols], ALU.add)
+            nc.scalar.activation(y0[:, cols], z0[:, cols], ACT.Sigmoid, bias=neg_th[:, 0:1])
+        for u in range(2):
+            cols = slice(u * HALF, (u + 1) * HALF)
+            nc.vector.tensor_copy(maps[0][:].indirect(half_offsets[u]), y0[:, cols])
+        nc.sync.dma_start(out[0, 0:P, :], maps[0][:])
+
+        a1_turned = ps.tile([P, CHUNKS, P], F32, name="a1_turned")
+        for c in range(CHUNKS):
+            cols = slice(c * P, (c + 1) * P)
+            nc.tensor.matmul_mx(
+                out=a1_turned[:, c, :],
+                lhsT=k_code[:, cols].bitcast(FP8X4),
+                lhsT_scale=k_scale[:, cols],
+                rhs=q_code[:, P:NQ].bitcast(FP8X4),
+                rhs_scale=q_scale[:, P:NQ],
+                start=True,
+                stop=True,
+            )
+        z1_turned = sb.tile([P, CHUNKS, P], F32, name="z1_turned")
+        for c in range(CHUNKS):
+            nc.scalar.activation(z1_turned[:, c, :], a1_turned[:, c, :], ACT.Identity, bias=kb_col[:, c : c + 1])
+        z1 = ps.tile([P, CHUNKS, P], F32, name="z1")
+        for c in range(CHUNKS):
+            nc.tensor.transpose(z1[:, c, :], z1_turned[:, c, :], ident[:])
+        y1 = sb.tile([P, N], F32, name="y1")
+        nc.scalar.activation(y1[:], z1[:].rearrange("p c n -> p (c n)"), ACT.Sigmoid, bias=neg_th[:, 1:2])
+        nc.vector.tensor_copy(maps[1][:].indirect(offsets[:]), y1[:])
+        nc.sync.dma_start(out[0, P:NQ, :], maps[1][:])

@@ -11,7 +11,6 @@ U16 = mybir.dt.uint16
 U8 = mybir.dt.uint8
 FP8X4 = mybir.dt.float8_e4m3fn_x4
 ACT = mybir.ActivationFunctionType
-ALU = mybir.AluOpType
 
 P = 128
 PACK = 4
@@ -41,16 +40,16 @@ def tile_attend_sigscat_topk_kernel(tc, qT, k_words, k_scales, kb, th, offs, out
         scale_pool = sb.tile([P, T // 4], I32, name="scale_pool")
         nc.vector.memset(scale_pool[:], 0)
         kb_pool = sb.tile([P, T], F32, name="kb_pool", tag="wide0")
-        nc.vector.memset(kb_pool[0:KB_ROW, :], 0.0)
+        nc.vector.memset(kb_pool[0:KB_ROW, :].bitcast(I32), 0)
         nc.sync.dma_start(kb_pool[KB_ROW:P, :], kb[0:1, :])
 
-        q_raw = sb.tile([P, PACK, NQ], F32, name="q_raw", tag="wide1")
+        q_raw = sb.tile([P, PACK, NQ], F32, name="q_raw")
         nc.sync.dma_start(q_raw[:], qT[0].rearrange("(p j) w -> p j w", j=PACK))
         for quad in range(4):
             nc.sync.dma_start(
                 scale_pool[32 * quad : 32 * quad + 4, :], k_scales[0, 4 * quad : 4 * quad + 4, :].bitcast(I32)
             )
-        word_pool = sb.tile([P, T], I32, name="word_pool")
+        word_pool = sb.tile([P, T], I32, name="word_pool", tag="wide1")
         nc.sync.dma_start(word_pool[:], k_words[0].rearrange("p t r -> p (t r)").bitcast(I32))
         th_sb = sb.tile([P, 2], F32, name="th_sb")
         with nc.allow_non_contiguous_dma(reason="one threshold a partition for each of the two query tiles"):
@@ -71,9 +70,6 @@ def tile_attend_sigscat_topk_kernel(tc, qT, k_words, k_scales, kb, th, offs, out
             nc.tensor.transpose(kb_turned[:, c, :], kb_listed[:, c * P : (c + 1) * P], ident[:])
         kb_col = sb.tile([P, CHUNKS], F32, name="kb_col")
         nc.scalar.copy(kb_col[:], kb_turned[:, :, KB_ROW])
-        kb_spread = ps.tile([P, CHUNKS, P], F32, name="kb_spread")
-        for c in range(CHUNKS):
-            nc.tensor.transpose(kb_spread[:, c, :], kb_col[:, c : c + 1].to_broadcast([P, P]), ident[:])
 
         q_bf = sb.tile([P, NQ, PACK], BF16, name="q_bf", align_bytes=64)
         q_code = sb.tile([P, NQ], U32, name="q_code", align_bytes=64)
@@ -89,62 +85,56 @@ def tile_attend_sigscat_topk_kernel(tc, qT, k_words, k_scales, kb, th, offs, out
                 in_=q_bf[:, rows, :].rearrange("p w j -> p (w j)"),
             )
 
-        kb_rows = sb.tile([P, N], F32, name="kb_rows")
-        nc.scalar.copy(kb_rows[:], kb_spread[:].rearrange("p c n -> p (c n)"))
-
-        maps = [sb.tile([P, T], F32, name="map%d" % h, tag="wide%d" % h) for h in range(2)]
-        for h in range(2):
-            for c0 in range(0, T, ZERO_PIECE):
-                nc.gpsimd.memset(maps[h][:, c0 : c0 + ZERO_PIECE], 0.0)
-
         k_code = sb.tile([P, N], U32, name="k_code", align_bytes=64)
         for u in range(2):
             cols = slice(u * HALF, (u + 1) * HALF)
             nc.vector.tensor_copy(k_code[:, cols], word_pool[:].bitcast(U32).indirect(half_offsets[u]))
 
+        maps = [sb.tile([P, T], F32, name="map%d" % h, tag="wide%d" % h) for h in range(2)]
+        for h in range(2):
+            for c0 in range(0, T, ZERO_PIECE):
+                nc.vector.memset(maps[h][:, c0 : c0 + ZERO_PIECE].bitcast(I32), 0)
+
         neg_th = sb.tile([P, 2], F32, name="neg_th")
         nc.scalar.mul(neg_th[:], th_sb[:], -1.0)
 
-        z0 = sb.tile([P, N], F32, name="z0")
-        y0 = sb.tile([P, N], F32, name="y0")
-        for u in range(2):
-            cols = slice(u * HALF, (u + 1) * HALF)
-            a0 = ps.tile([P, HALF], F32, name="a0_%d" % u)
-            nc.tensor.matmul_mx(
-                out=a0[:],
-                lhsT=q_code[:, 0:P].bitcast(FP8X4),
-                lhsT_scale=q_scale[:, 0:P],
-                rhs=k_code[:, cols].bitcast(FP8X4),
-                rhs_scale=k_scale[:, cols],
-                start=True,
-                stop=True,
-            )
-            nc.vector.tensor_tensor(z0[:, cols], a0[:], kb_rows[:, cols], ALU.add)
-            nc.scalar.activation(y0[:, cols], z0[:, cols], ACT.Sigmoid, bias=neg_th[:, 0:1])
-        for u in range(2):
-            cols = slice(u * HALF, (u + 1) * HALF)
-            nc.vector.tensor_copy(maps[0][:].indirect(half_offsets[u]), y0[:, cols])
-        nc.sync.dma_start(out[0, 0:P, :], maps[0][:])
+        z_turned = sb.tile([P, 2, CHUNKS, P], F32, name="z_turned")
+        y = sb.tile([P, 2, N], F32, name="y")
 
-        a1_turned = ps.tile([P, CHUNKS, P], F32, name="a1_turned")
-        for c in range(CHUNKS):
-            cols = slice(c * P, (c + 1) * P)
-            nc.tensor.matmul_mx(
-                out=a1_turned[:, c, :],
-                lhsT=k_code[:, cols].bitcast(FP8X4),
-                lhsT_scale=k_scale[:, cols],
-                rhs=q_code[:, P:NQ].bitcast(FP8X4),
-                rhs_scale=q_scale[:, P:NQ],
-                start=True,
-                stop=True,
-            )
-        z1_turned = sb.tile([P, CHUNKS, P], F32, name="z1_turned")
-        for c in range(CHUNKS):
-            nc.scalar.activation(z1_turned[:, c, :], a1_turned[:, c, :], ACT.Identity, bias=kb_col[:, c : c + 1])
-        z1 = ps.tile([P, CHUNKS, P], F32, name="z1")
-        for c in range(CHUNKS):
-            nc.tensor.transpose(z1[:, c, :], z1_turned[:, c, :], ident[:])
-        y1 = sb.tile([P, N], F32, name="y1")
-        nc.scalar.activation(y1[:], z1[:].rearrange("p c n -> p (c n)"), ACT.Sigmoid, bias=neg_th[:, 1:2])
-        nc.vector.tensor_copy(maps[1][:].indirect(offsets[:]), y1[:])
+        def scores(h, u):
+            rows = slice(h * P, (h + 1) * P)
+            a_turned = ps.tile([P, 2, P], F32, name="a_turned%d%d" % (h, u))
+            for i in range(2):
+                c = 2 * u + i
+                cols = slice(c * P, (c + 1) * P)
+                nc.tensor.matmul_mx(
+                    out=a_turned[:, i, :],
+                    lhsT=k_code[:, cols].bitcast(FP8X4),
+                    lhsT_scale=k_scale[:, cols],
+                    rhs=q_code[:, rows].bitcast(FP8X4),
+                    rhs_scale=q_scale[:, rows],
+                    start=True,
+                    stop=True,
+                )
+            for i in range(2):
+                c = 2 * u + i
+                nc.scalar.activation(z_turned[:, h, c, :], a_turned[:, i, :], ACT.Identity, bias=kb_col[:, c : c + 1])
+
+        def gate(h, chunks):
+            z = ps.tile([P, len(chunks), P], F32, name="z%d%d" % (h, chunks[0]))
+            for i, c in enumerate(chunks):
+                nc.tensor.transpose(z[:, i, :], z_turned[:, h, c, :], ident[:])
+            cols = slice(chunks[0] * P, (chunks[-1] + 1) * P)
+            nc.scalar.activation(y[:, h, cols], z[:].rearrange("p c n -> p (c n)"), ACT.Sigmoid, bias=neg_th[:, h : h + 1])
+
+        for u in range(2):
+            scores(0, u)
+            gate(0, [2 * u, 2 * u + 1])
+        for u in range(2):
+            nc.vector.tensor_copy(maps[0][:].indirect(half_offsets[u]), y[:, 0, u * HALF : (u + 1) * HALF])
+        nc.sync.dma_start(out[0, 0:P, :], maps[0][:])
+        for u in range(2):
+            scores(1, u)
+        gate(1, [0, 1, 2, 3])
+        nc.vector.tensor_copy(maps[1][:].indirect(offsets[:]), y[:, 1, :])
         nc.sync.dma_start(out[0, P:NQ, :], maps[1][:])

@@ -21,10 +21,13 @@ D = 512
 HALF = N // 2
 CHUNKS = N // P
 KB_ROW = P - 1
-ZERO_PIECE = 512
 
 FLOPS = 2 * NQ * N * D
 BYTES = 4 * D * NQ + D * T + 16 * T + 4 * T + 4 * NQ + 2 * P * (N // 16) + 4 * NQ * T
+
+
+def odd_halves(width):
+    return [slice(0, width // 2 - 1), slice(width // 2 - 1, width)]
 
 
 def tile_attend_sigscat_topk_kernel(tc, qT, k_words, k_scales, kb, th, offs, out):
@@ -38,9 +41,11 @@ def tile_attend_sigscat_topk_kernel(tc, qT, k_words, k_scales, kb, th, offs, out
         half_offsets = [offsets[:, u * (HALF // 16) : (u + 1) * (HALF // 16)] for u in range(2)]
 
         scale_pool = sb.tile([P, T // 4], I32, name="scale_pool")
-        nc.vector.memset(scale_pool[:], 0)
-        kb_pool = sb.tile([P, T], F32, name="kb_pool", tag="wide0")
-        nc.vector.memset(kb_pool[0:KB_ROW, :].bitcast(I32), 0)
+        for cols in odd_halves(T // 4):
+            nc.vector.memset(scale_pool[:, cols], 0)
+        kb_pool = sb.tile([P, T], F32, name="kb_pool")
+        for cols in odd_halves(T):
+            nc.vector.memset(kb_pool[0:KB_ROW, cols].bitcast(I32), 0)
         nc.sync.dma_start(kb_pool[KB_ROW:P, :], kb[0:1, :])
 
         q_raw = sb.tile([P, PACK, NQ], F32, name="q_raw")
@@ -57,6 +62,8 @@ def tile_attend_sigscat_topk_kernel(tc, qT, k_words, k_scales, kb, th, offs, out
 
         ident = sb.tile([P, P], F32, name="ident")
         make_identity(nc, ident[:])
+        map0 = sb.tile([P, T], F32, name="map0")
+        nc.gpsimd.memset(map0[:], 0.0)
         warm = sb.tile([P, 1], F32, name="warm")
         nc.scalar.activation(warm[:], ident[:, 0:1], ACT.Sigmoid)
 
@@ -65,7 +72,7 @@ def tile_attend_sigscat_topk_kernel(tc, qT, k_words, k_scales, kb, th, offs, out
         k_scale = sb.tile([P, N], U8, name="k_scale", align_bytes=64)
         nc.vector.tensor_copy(k_scale[:], scale_pool[:].bitcast(U8).indirect(offsets[:]))
 
-        kb_turned = ps.tile([P, CHUNKS, P], F32, name="kb_turned")
+        kb_turned = ps.tile([P, CHUNKS, P], F32, name="kb_turned", tag="kb_turned")
         for c in range(CHUNKS):
             nc.tensor.transpose(kb_turned[:, c, :], kb_listed[:, c * P : (c + 1) * P], ident[:])
         kb_col = sb.tile([P, CHUNKS], F32, name="kb_col")
@@ -90,10 +97,8 @@ def tile_attend_sigscat_topk_kernel(tc, qT, k_words, k_scales, kb, th, offs, out
             cols = slice(u * HALF, (u + 1) * HALF)
             nc.vector.tensor_copy(k_code[:, cols], word_pool[:].bitcast(U32).indirect(half_offsets[u]))
 
-        maps = [sb.tile([P, T], F32, name="map%d" % h, tag="wide%d" % h) for h in range(2)]
-        for h in range(2):
-            for c0 in range(0, T, ZERO_PIECE):
-                nc.vector.memset(maps[h][:, c0 : c0 + ZERO_PIECE].bitcast(I32), 0)
+        map1 = sb.tile([P, T], F32, name="map1", tag="wide1")
+        nc.vector.memset(map1[:].bitcast(I32), 0)
 
         neg_th = sb.tile([P, 2], F32, name="neg_th")
         nc.scalar.mul(neg_th[:], th_sb[:], -1.0)
@@ -101,40 +106,44 @@ def tile_attend_sigscat_topk_kernel(tc, qT, k_words, k_scales, kb, th, offs, out
         z_turned = sb.tile([P, 2, CHUNKS, P], F32, name="z_turned")
         y = sb.tile([P, 2, N], F32, name="y")
 
-        def scores(h, u):
+        def score(dst, h, c):
             rows = slice(h * P, (h + 1) * P)
-            a_turned = ps.tile([P, 2, P], F32, name="a_turned%d%d" % (h, u))
-            for i in range(2):
-                c = 2 * u + i
-                cols = slice(c * P, (c + 1) * P)
-                nc.tensor.matmul_mx(
-                    out=a_turned[:, i, :],
-                    lhsT=k_code[:, cols].bitcast(FP8X4),
-                    lhsT_scale=k_scale[:, cols],
-                    rhs=q_code[:, rows].bitcast(FP8X4),
-                    rhs_scale=q_scale[:, rows],
-                    start=True,
-                    stop=True,
-                )
-            for i in range(2):
-                c = 2 * u + i
-                nc.scalar.activation(z_turned[:, h, c, :], a_turned[:, i, :], ACT.Identity, bias=kb_col[:, c : c + 1])
+            cols = slice(c * P, (c + 1) * P)
+            nc.tensor.matmul_mx(
+                out=dst,
+                lhsT=k_code[:, cols].bitcast(FP8X4),
+                lhsT_scale=k_scale[:, cols],
+                rhs=q_code[:, rows].bitcast(FP8X4),
+                rhs_scale=q_scale[:, rows],
+                start=True,
+                stop=True,
+            )
 
-        def gate(h, chunks):
-            z = ps.tile([P, len(chunks), P], F32, name="z%d%d" % (h, chunks[0]))
+        def add_kb(src, h, c):
+            nc.scalar.activation(z_turned[:, h, c, :], src, ACT.Identity, bias=kb_col[:, c : c + 1])
+
+        def gate(h, chunks, tag):
+            z = ps.tile([P, len(chunks), P], F32, name="z%d%d" % (h, chunks[0]), tag=tag)
             for i, c in enumerate(chunks):
                 nc.tensor.transpose(z[:, i, :], z_turned[:, h, c, :], ident[:])
             cols = slice(chunks[0] * P, (chunks[-1] + 1) * P)
             nc.scalar.activation(y[:, h, cols], z[:].rearrange("p c n -> p (c n)"), ACT.Sigmoid, bias=neg_th[:, h : h + 1])
 
         for u in range(2):
-            scores(0, u)
-            gate(0, [2 * u, 2 * u + 1])
+            for c in (2 * u, 2 * u + 1):
+                a0 = ps.tile([P, P], F32, name="a0_%d" % c, tag="score%d" % c)
+                score(a0[:], 0, c)
+                add_kb(a0[:], 0, c)
+            gate(0, [2 * u, 2 * u + 1], "gate%d" % u)
         for u in range(2):
-            nc.vector.tensor_copy(maps[0][:].indirect(half_offsets[u]), y[:, 0, u * HALF : (u + 1) * HALF])
-        nc.sync.dma_start(out[0, 0:P, :], maps[0][:])
+            nc.vector.tensor_copy(map0[:].indirect(half_offsets[u]), y[:, 0, u * HALF : (u + 1) * HALF])
+        nc.sync.dma_start(out[0, 0:P, :], map0[:])
         for u in range(2):
-            scores(1, u)
-        gate(1, [0, 1, 2, 3])
-        nc.vector.tensor_copy(maps[1][:].indirect(offsets[:]), y[:, 1, :])
-        nc.sync.dma_start(out[0, P:NQ, :], maps[1][:])
+            a1 = ps.tile([P, 2, P], F32, name="a1_%d" % u, tag="score%d" % (2 * u + 1))
+            for i in range(2):
+                score(a1[:, i, :], 1, 2 * u + i)
+            for i in range(2):
+                add_kb(a1[:, i, :], 1, 2 * u + i)
+        gate(1, [0, 1, 2, 3], "kb_turned")
+        nc.vector.tensor_copy(map1[:].indirect(offsets[:]), y[:, 1, :])
+        nc.sync.dma_start(out[0, P:NQ, :], map1[:])

@@ -11,6 +11,7 @@ U16 = mybir.dt.uint16
 U8 = mybir.dt.uint8
 FP8X4 = mybir.dt.float8_e4m3fn_x4
 ACT = mybir.ActivationFunctionType
+ALU = mybir.AluOpType
 
 P = 128
 PACK = 4
@@ -26,8 +27,12 @@ FLOPS = 2 * NQ * N * D
 BYTES = 4 * D * NQ + D * T + 16 * T + 4 * T + 4 * NQ + 2 * P * (N // 16) + 4 * NQ * T
 
 
-def odd_halves(width):
-    return [slice(0, width // 2 - 1), slice(width // 2 - 1, width)]
+KB_SPLIT = 960
+
+
+def odd_halves(lo, hi):
+    mid = (lo + hi) // 2 - 1
+    return [slice(lo, mid), slice(mid, hi)]
 
 
 def tile_attend_sigscat_topk_kernel(tc, qT, k_words, k_scales, kb, th, offs, out):
@@ -41,27 +46,30 @@ def tile_attend_sigscat_topk_kernel(tc, qT, k_words, k_scales, kb, th, offs, out
         half_offsets = [offsets[:, u * (HALF // 16) : (u + 1) * (HALF // 16)] for u in range(2)]
 
         scale_pool = sb.tile([P, T // 4], I32, name="scale_pool")
-        for cols in odd_halves(T // 4):
+        for cols in odd_halves(0, T // 4):
             nc.vector.memset(scale_pool[:, cols], 0)
         kb_pool = sb.tile([P, T], F32, name="kb_pool")
-        for cols in odd_halves(T):
+        for cols in odd_halves(0, KB_SPLIT):
             nc.vector.memset(kb_pool[0:KB_ROW, cols].bitcast(I32), 0)
         nc.sync.dma_start(kb_pool[KB_ROW:P, :], kb[0:1, :])
 
-        q_raw = sb.tile([P, PACK, NQ], F32, name="q_raw")
-        nc.sync.dma_start(q_raw[:], qT[0].rearrange("(p j) w -> p j w", j=PACK))
+        q_rows = qT[0].rearrange("(p j) w -> p j w", j=PACK)
+        q_raw = [sb.tile([P, PACK, P], F32, name="q_raw%d" % h) for h in range(2)]
+        nc.sync.dma_start(q_raw[0][:], q_rows[:, :, 0:P])
         for quad in range(4):
             nc.sync.dma_start(
                 scale_pool[32 * quad : 32 * quad + 4, :], k_scales[0, 4 * quad : 4 * quad + 4, :].bitcast(I32)
             )
-        word_pool = sb.tile([P, T], I32, name="word_pool", tag="wide1")
+        word_pool = sb.tile([P, T], I32, name="word_pool")
         nc.sync.dma_start(word_pool[:], k_words[0].rearrange("p t r -> p (t r)").bitcast(I32))
         th_sb = sb.tile([P, 2], F32, name="th_sb")
         with nc.allow_non_contiguous_dma(reason="one threshold a partition for each of the two query tiles"):
             nc.sync.dma_start(th_sb[:], th[0, :, 0].rearrange("(h p) -> p h", p=P))
+        nc.sync.dma_start(q_raw[1][:], q_rows[:, :, P:NQ])
 
         ident = sb.tile([P, P], F32, name="ident")
         make_identity(nc, ident[:])
+        nc.gpsimd.memset(kb_pool[0:KB_ROW, KB_SPLIT:T], 0.0)
         map0 = sb.tile([P, T], F32, name="map0")
         nc.gpsimd.memset(map0[:], 0.0)
         warm = sb.tile([P, 1], F32, name="warm")
@@ -78,30 +86,36 @@ def tile_attend_sigscat_topk_kernel(tc, qT, k_words, k_scales, kb, th, offs, out
         kb_col = sb.tile([P, CHUNKS], F32, name="kb_col")
         nc.scalar.copy(kb_col[:], kb_turned[:, :, KB_ROW])
 
-        q_bf = sb.tile([P, NQ, PACK], BF16, name="q_bf", align_bytes=64)
+        q_bf = [
+            sb.tile([P, P, PACK], BF16, name="q_bf0", align_bytes=64),
+            sb.tile([P, P, PACK], BF16, name="q_bf1", tag="wide1", align_bytes=64),
+        ]
         q_code = sb.tile([P, NQ], U32, name="q_code", align_bytes=64)
         q_scale = sb.tile([P, NQ], U8, name="q_scale", align_bytes=64)
-        for h in range(2):
-            rows = slice(h * P, (h + 1) * P)
-            nc.scalar.copy(q_bf[:, rows, :], q_raw[:, :, rows].rearrange("p j w -> p w j"))
-        for h in range(2):
+
+        def quantise(h):
             rows = slice(h * P, (h + 1) * P)
             nc.vector.quantize_mx(
                 out=q_code[:, rows].bitcast(FP8X4),
                 scales=q_scale[:, rows],
-                in_=q_bf[:, rows, :].rearrange("p w j -> p (w j)"),
+                in_=q_bf[h][:].rearrange("p w j -> p (w j)"),
             )
+
+        nc.scalar.copy(q_bf[0][:], q_raw[0][:].rearrange("p j w -> p w j"))
+        quantise(0)
 
         k_code = sb.tile([P, N], U32, name="k_code", align_bytes=64)
         for u in range(2):
             cols = slice(u * HALF, (u + 1) * HALF)
             nc.vector.tensor_copy(k_code[:, cols], word_pool[:].bitcast(U32).indirect(half_offsets[u]))
 
-        map1 = sb.tile([P, T], F32, name="map1", tag="wide1")
-        nc.vector.memset(map1[:].bitcast(I32), 0)
+        nc.vector.tensor_copy(q_bf[1][:], q_raw[1][:].rearrange("p j w -> p w j"))
+        quantise(1)
 
         neg_th = sb.tile([P, 2], F32, name="neg_th")
-        nc.scalar.mul(neg_th[:], th_sb[:], -1.0)
+        nc.gpsimd.tensor_scalar(neg_th[:], th_sb[:], -1.0, 0.0, ALU.mult, ALU.add)
+        map1 = sb.tile([P, T], F32, name="map1", tag="wide1", align_bytes=64)
+        nc.gpsimd.memset(map1[:], 0.0)
 
         z_turned = sb.tile([P, 2, CHUNKS, P], F32, name="z_turned")
         y = sb.tile([P, 2, N], F32, name="y")
@@ -129,21 +143,25 @@ def tile_attend_sigscat_topk_kernel(tc, qT, k_words, k_scales, kb, th, offs, out
             cols = slice(chunks[0] * P, (chunks[-1] + 1) * P)
             nc.scalar.activation(y[:, h, cols], z[:].rearrange("p c n -> p (c n)"), ACT.Sigmoid, bias=neg_th[:, h : h + 1])
 
-        for u in range(2):
-            for c in (2 * u, 2 * u + 1):
-                a0 = ps.tile([P, P], F32, name="a0_%d" % c, tag="score%d" % c)
-                score(a0[:], 0, c)
-                add_kb(a0[:], 0, c)
-            gate(0, [2 * u, 2 * u + 1], "gate%d" % u)
+        def score_pair(h, u, tag):
+            a = ps.tile([P, 2, P], F32, name="a%d_%d" % (h, u), tag=tag)
+            for i in range(2):
+                score(a[:, i, :], h, 2 * u + i)
+            for i in range(2):
+                add_kb(a[:, i, :], h, 2 * u + i)
+
+        for c in range(2):
+            a0 = ps.tile([P, P], F32, name="a0_c%d" % c, tag="score%d" % c)
+            score(a0[:], 0, c)
+            add_kb(a0[:], 0, c)
+        gate(0, [0, 1], "gate0")
+        score_pair(0, 1, "score1")
+        gate(0, [2, 3], "gate1")
         for u in range(2):
             nc.vector.tensor_copy(map0[:].indirect(half_offsets[u]), y[:, 0, u * HALF : (u + 1) * HALF])
         nc.sync.dma_start(out[0, 0:P, :], map0[:])
-        for u in range(2):
-            a1 = ps.tile([P, 2, P], F32, name="a1_%d" % u, tag="score%d" % (2 * u + 1))
-            for i in range(2):
-                score(a1[:, i, :], 1, 2 * u + i)
-            for i in range(2):
-                add_kb(a1[:, i, :], 1, 2 * u + i)
+        score_pair(1, 0, "gate0")
+        score_pair(1, 1, "score1")
         gate(1, [0, 1, 2, 3], "kb_turned")
         nc.vector.tensor_copy(map1[:].indirect(offsets[:]), y[:, 1, :])
         nc.sync.dma_start(out[0, P:NQ, :], map1[:])

@@ -22,12 +22,10 @@ D = 512
 HALF = N // 2
 CHUNKS = N // P
 KB_ROW = P - 1
+KB_SPLIT = 1472
 
 FLOPS = 2 * NQ * N * D
 BYTES = 4 * D * NQ + D * T + 16 * T + 4 * T + 4 * NQ + 2 * P * (N // 16) + 4 * NQ * T
-
-
-KB_SPLIT = 960
 
 
 def odd_halves(lo, hi):
@@ -44,10 +42,10 @@ def tile_attend_sigscat_topk_kernel(tc, qT, k_words, k_scales, kb, th, offs, out
         offsets = sb.tile([P, N // 16], U16, name="offsets")
         nc.sync.dma_start(offsets[:], offs)
         half_offsets = [offsets[:, u * (HALF // 16) : (u + 1) * (HALF // 16)] for u in range(2)]
+        halves = [slice(u * HALF, (u + 1) * HALF) for u in range(2)]
 
         scale_pool = sb.tile([P, T // 4], I32, name="scale_pool")
-        for cols in odd_halves(0, T // 4):
-            nc.vector.memset(scale_pool[:, cols], 0)
+        nc.gpsimd.memset(scale_pool[:], 0)
         kb_pool = sb.tile([P, T], F32, name="kb_pool")
         for cols in odd_halves(0, KB_SPLIT):
             nc.vector.memset(kb_pool[0:KB_ROW, cols].bitcast(I32), 0)
@@ -69,22 +67,31 @@ def tile_attend_sigscat_topk_kernel(tc, qT, k_words, k_scales, kb, th, offs, out
 
         ident = sb.tile([P, P], F32, name="ident")
         make_identity(nc, ident[:])
-        nc.gpsimd.memset(kb_pool[0:KB_ROW, KB_SPLIT:T], 0.0)
         map0 = sb.tile([P, T], F32, name="map0")
+        nc.gpsimd.memset(kb_pool[0:KB_ROW, KB_SPLIT:T], 0.0)
         nc.gpsimd.memset(map0[:], 0.0)
         warm = sb.tile([P, 1], F32, name="warm")
         nc.scalar.activation(warm[:], ident[:, 0:1], ACT.Sigmoid)
 
         kb_listed = sb.tile([P, N], F32, name="kb_listed")
-        nc.vector.tensor_copy(kb_listed[:], kb_pool[:].indirect(offsets[:]))
+        for u in range(2):
+            nc.vector.tensor_copy(kb_listed[:, halves[u]], kb_pool[:].indirect(half_offsets[u]))
         k_scale = sb.tile([P, N], U8, name="k_scale", align_bytes=64)
         nc.vector.tensor_copy(k_scale[:], scale_pool[:].bitcast(U8).indirect(offsets[:]))
 
-        kb_turned = ps.tile([P, CHUNKS, P], F32, name="kb_turned", tag="kb_turned")
-        for c in range(CHUNKS):
-            nc.tensor.transpose(kb_turned[:, c, :], kb_listed[:, c * P : (c + 1) * P], ident[:])
         kb_col = sb.tile([P, CHUNKS], F32, name="kb_col")
-        nc.scalar.copy(kb_col[:], kb_turned[:, :, KB_ROW])
+        kb_rows = sb.tile([P, N], F32, name="kb_rows")
+        for u in range(2):
+            kb_turned = ps.tile([P, 2, P], F32, name="kb_turned%d" % u, tag="kb_turned%d" % u)
+            for i in range(2):
+                c = 2 * u + i
+                nc.tensor.transpose(kb_turned[:, i, :], kb_listed[:, c * P : (c + 1) * P], ident[:])
+            nc.scalar.copy(kb_col[:, 2 * u : 2 * u + 2], kb_turned[:, :, KB_ROW])
+            kb_spread = ps.tile([P, 2, P], F32, name="kb_spread%d" % u, tag="kb_spread%d" % u)
+            for i in range(2):
+                c = 2 * u + i
+                nc.tensor.transpose(kb_spread[:, i, :], kb_col[:, c : c + 1].to_broadcast([P, P]), ident[:])
+            nc.scalar.copy(kb_rows[:, halves[u]], kb_spread[:].rearrange("p c n -> p (c n)"))
 
         q_bf = [
             sb.tile([P, P, PACK], BF16, name="q_bf0", align_bytes=64),
@@ -103,35 +110,35 @@ def tile_attend_sigscat_topk_kernel(tc, qT, k_words, k_scales, kb, th, offs, out
 
         nc.scalar.copy(q_bf[0][:], q_raw[0][:].rearrange("p j w -> p w j"))
         quantise(0)
+        neg_th = sb.tile([P, 2], F32, name="neg_th")
+        nc.gpsimd.tensor_scalar(neg_th[:], th_sb[:], -1.0, 0.0, ALU.mult, ALU.add)
 
         k_code = sb.tile([P, N], U32, name="k_code", align_bytes=64)
         for u in range(2):
-            cols = slice(u * HALF, (u + 1) * HALF)
-            nc.vector.tensor_copy(k_code[:, cols], word_pool[:].bitcast(U32).indirect(half_offsets[u]))
-
-        nc.vector.tensor_copy(q_bf[1][:], q_raw[1][:].rearrange("p j w -> p w j"))
-        quantise(1)
-
-        neg_th = sb.tile([P, 2], F32, name="neg_th")
-        nc.gpsimd.tensor_scalar(neg_th[:], th_sb[:], -1.0, 0.0, ALU.mult, ALU.add)
-        map1 = sb.tile([P, T], F32, name="map1", tag="wide1", align_bytes=64)
-        nc.gpsimd.memset(map1[:], 0.0)
+            nc.vector.tensor_copy(k_code[:, halves[u]], word_pool[:].bitcast(U32).indirect(half_offsets[u]))
 
         z_turned = sb.tile([P, 2, CHUNKS, P], F32, name="z_turned")
         y = sb.tile([P, 2, N], F32, name="y")
 
-        def score(dst, h, c):
-            rows = slice(h * P, (h + 1) * P)
-            cols = slice(c * P, (c + 1) * P)
+        def product(dst, stationary, moving):
             nc.tensor.matmul_mx(
                 out=dst,
-                lhsT=k_code[:, cols].bitcast(FP8X4),
-                lhsT_scale=k_scale[:, cols],
-                rhs=q_code[:, rows].bitcast(FP8X4),
-                rhs_scale=q_scale[:, rows],
+                lhsT=stationary[0].bitcast(FP8X4),
+                lhsT_scale=stationary[1],
+                rhs=moving[0].bitcast(FP8X4),
+                rhs_scale=moving[1],
                 start=True,
                 stop=True,
             )
+
+        def queries(h):
+            return q_code[:, h * P : (h + 1) * P], q_scale[:, h * P : (h + 1) * P]
+
+        def keys(cols):
+            return k_code[:, cols], k_scale[:, cols]
+
+        def score(dst, h, c):
+            product(dst, keys(slice(c * P, (c + 1) * P)), queries(h))
 
         def add_kb(src, h, c):
             nc.scalar.activation(z_turned[:, h, c, :], src, ACT.Identity, bias=kb_col[:, c : c + 1])
@@ -150,18 +157,21 @@ def tile_attend_sigscat_topk_kernel(tc, qT, k_words, k_scales, kb, th, offs, out
             for i in range(2):
                 add_kb(a[:, i, :], h, 2 * u + i)
 
-        for c in range(2):
-            a0 = ps.tile([P, P], F32, name="a0_c%d" % c, tag="score%d" % c)
-            score(a0[:], 0, c)
-            add_kb(a0[:], 0, c)
-        gate(0, [0, 1], "gate0")
-        score_pair(0, 1, "score1")
-        gate(0, [2, 3], "gate1")
+        z0 = sb.tile([P, N], F32, name="z0")
         for u in range(2):
-            nc.vector.tensor_copy(map0[:].indirect(half_offsets[u]), y[:, 0, u * HALF : (u + 1) * HALF])
+            a0 = ps.tile([P, HALF], F32, name="a0_%d" % u, tag="score%d" % u)
+            product(a0[:], queries(0), keys(halves[u]))
+            nc.vector.tensor_tensor(z0[:, halves[u]], a0[:], kb_rows[:, halves[u]], ALU.add)
+            nc.scalar.activation(y[:, 0, halves[u]], z0[:, halves[u]], ACT.Sigmoid, bias=neg_th[:, 0:1])
+        nc.scalar.copy(q_bf[1][:], q_raw[1][:].rearrange("p j w -> p w j"))
+        quantise(1)
+        map1 = sb.tile([P, T], F32, name="map1", tag="wide1", align_bytes=64)
+        nc.gpsimd.memset(map1[:], 0.0)
+        for u in range(2):
+            nc.vector.tensor_copy(map0[:].indirect(half_offsets[u]), y[:, 0, halves[u]])
         nc.sync.dma_start(out[0, 0:P, :], map0[:])
-        score_pair(1, 0, "gate0")
-        score_pair(1, 1, "score1")
-        gate(1, [0, 1, 2, 3], "kb_turned")
+        score_pair(1, 0, "score2")
+        score_pair(1, 1, "score3")
+        gate(1, [0, 1, 2, 3], "kb_turned0")
         nc.vector.tensor_copy(map1[:].indirect(offsets[:]), y[:, 1, :])
         nc.sync.dma_start(out[0, P:NQ, :], map1[:])

@@ -60,10 +60,10 @@ def tile_attend_sigscat_topk_kernel(tc, qT, k_words, k_scales, kb, th, offs, out
             )
         word_pool = sb.tile([P, T], I32, name="word_pool")
         nc.sync.dma_start(word_pool[:], k_words[0].rearrange("p t r -> p (t r)").bitcast(I32))
+        nc.sync.dma_start(q_raw[1][:], q_rows[:, :, P:NQ])
         th_sb = sb.tile([P, 2], F32, name="th_sb")
         with nc.allow_non_contiguous_dma(reason="one threshold a partition for each of the two query tiles"):
             nc.sync.dma_start(th_sb[:], th[0, :, 0].rearrange("(h p) -> p h", p=P))
-        nc.sync.dma_start(q_raw[1][:], q_rows[:, :, P:NQ])
 
         ident = sb.tile([P, P], F32, name="ident")
         make_identity(nc, ident[:])
@@ -161,8 +161,12 @@ def tile_attend_sigscat_topk_kernel(tc, qT, k_words, k_scales, kb, th, offs, out
         for u in range(2):
             a0 = ps.tile([P, HALF], F32, name="a0_%d" % u, tag="score%d" % u)
             product(a0[:], queries(0), keys(halves[u]))
-            nc.vector.tensor_tensor(z0[:, halves[u]], a0[:], kb_rows[:, halves[u]], ALU.add)
-            nc.scalar.activation(y[:, 0, halves[u]], z0[:, halves[u]], ACT.Sigmoid, bias=neg_th[:, 0:1])
+            pieces = 2 - u
+            for i in range(pieces):
+                width = HALF // pieces
+                cols = slice(u * HALF + i * width, u * HALF + (i + 1) * width)
+                nc.vector.tensor_tensor(z0[:, cols], a0[:, i * width : (i + 1) * width], kb_rows[:, cols], ALU.add)
+                nc.scalar.activation(y[:, 0, cols], z0[:, cols], ACT.Sigmoid, bias=neg_th[:, 0:1])
         nc.scalar.copy(q_bf[1][:], q_raw[1][:].rearrange("p j w -> p w j"))
         quantise(1)
         map1 = sb.tile([P, T], F32, name="map1", tag="wide1", align_bytes=64)

@@ -28,9 +28,8 @@ FLOPS = 2 * NQ * N * D
 BYTES = 4 * D * NQ + D * T + 16 * T + 4 * T + 4 * NQ + 2 * P * (N // 16) + 4 * NQ * T
 
 
-def odd_halves(lo, hi):
-    mid = (lo + hi) // 2 - 1
-    return [slice(lo, mid), slice(mid, hi)]
+def odd_pieces(width):
+    return [slice(0, width // 2 - 1), slice(width // 2 - 1, width)]
 
 
 def tile_attend_sigscat_topk_kernel(tc, qT, k_words, k_scales, kb, th, offs, out):
@@ -47,7 +46,7 @@ def tile_attend_sigscat_topk_kernel(tc, qT, k_words, k_scales, kb, th, offs, out
         scale_pool = sb.tile([P, T // 4], I32, name="scale_pool")
         nc.gpsimd.memset(scale_pool[:], 0)
         kb_pool = sb.tile([P, T], F32, name="kb_pool")
-        for cols in odd_halves(0, KB_SPLIT):
+        for cols in odd_pieces(KB_SPLIT):
             nc.vector.memset(kb_pool[0:KB_ROW, cols].bitcast(I32), 0)
         nc.sync.dma_start(kb_pool[KB_ROW:P, :], kb[0:1, :])
 
@@ -102,13 +101,13 @@ def tile_attend_sigscat_topk_kernel(tc, qT, k_words, k_scales, kb, th, offs, out
 
         def quantise(h):
             rows = slice(h * P, (h + 1) * P)
+            nc.scalar.copy(q_bf[h][:], q_raw[h][:].rearrange("p j w -> p w j"))
             nc.vector.quantize_mx(
                 out=q_code[:, rows].bitcast(FP8X4),
                 scales=q_scale[:, rows],
                 in_=q_bf[h][:].rearrange("p w j -> p (w j)"),
             )
 
-        nc.scalar.copy(q_bf[0][:], q_raw[0][:].rearrange("p j w -> p w j"))
         quantise(0)
         neg_th = sb.tile([P, 2], F32, name="neg_th")
         nc.gpsimd.tensor_scalar(neg_th[:], th_sb[:], -1.0, 0.0, ALU.mult, ALU.add)
@@ -117,7 +116,7 @@ def tile_attend_sigscat_topk_kernel(tc, qT, k_words, k_scales, kb, th, offs, out
         for u in range(2):
             nc.vector.tensor_copy(k_code[:, halves[u]], word_pool[:].bitcast(U32).indirect(half_offsets[u]))
 
-        z_turned = sb.tile([P, 2, CHUNKS, P], F32, name="z_turned")
+        z1_turned = sb.tile([P, CHUNKS, P], F32, name="z1_turned")
         y = sb.tile([P, 2, N], F32, name="y")
 
         def product(dst, stationary, moving):
@@ -137,45 +136,34 @@ def tile_attend_sigscat_topk_kernel(tc, qT, k_words, k_scales, kb, th, offs, out
         def keys(cols):
             return k_code[:, cols], k_scale[:, cols]
 
-        def score(dst, h, c):
-            product(dst, keys(slice(c * P, (c + 1) * P)), queries(h))
-
-        def add_kb(src, h, c):
-            nc.scalar.activation(z_turned[:, h, c, :], src, ACT.Identity, bias=kb_col[:, c : c + 1])
-
-        def gate(h, chunks, tag):
-            z = ps.tile([P, len(chunks), P], F32, name="z%d%d" % (h, chunks[0]), tag=tag)
-            for i, c in enumerate(chunks):
-                nc.tensor.transpose(z[:, i, :], z_turned[:, h, c, :], ident[:])
-            cols = slice(chunks[0] * P, (chunks[-1] + 1) * P)
-            nc.scalar.activation(y[:, h, cols], z[:].rearrange("p c n -> p (c n)"), ACT.Sigmoid, bias=neg_th[:, h : h + 1])
-
-        def score_pair(h, u, tag):
-            a = ps.tile([P, 2, P], F32, name="a%d_%d" % (h, u), tag=tag)
-            for i in range(2):
-                score(a[:, i, :], h, 2 * u + i)
-            for i in range(2):
-                add_kb(a[:, i, :], h, 2 * u + i)
-
         z0 = sb.tile([P, N], F32, name="z0")
         for u in range(2):
             a0 = ps.tile([P, HALF], F32, name="a0_%d" % u, tag="score%d" % u)
             product(a0[:], queries(0), keys(halves[u]))
-            pieces = 2 - u
+            pieces = 2 if u == 0 else 1
+            width = HALF // pieces
             for i in range(pieces):
-                width = HALF // pieces
                 cols = slice(u * HALF + i * width, u * HALF + (i + 1) * width)
                 nc.vector.tensor_tensor(z0[:, cols], a0[:, i * width : (i + 1) * width], kb_rows[:, cols], ALU.add)
                 nc.scalar.activation(y[:, 0, cols], z0[:, cols], ACT.Sigmoid, bias=neg_th[:, 0:1])
-        nc.scalar.copy(q_bf[1][:], q_raw[1][:].rearrange("p j w -> p w j"))
         quantise(1)
         map1 = sb.tile([P, T], F32, name="map1", tag="wide1", align_bytes=64)
         nc.gpsimd.memset(map1[:], 0.0)
         for u in range(2):
             nc.vector.tensor_copy(map0[:].indirect(half_offsets[u]), y[:, 0, halves[u]])
         nc.sync.dma_start(out[0, 0:P, :], map0[:])
-        score_pair(1, 0, "score2")
-        score_pair(1, 1, "score3")
-        gate(1, [0, 1, 2, 3], "kb_turned0")
+
+        for u in range(2):
+            a1 = ps.tile([P, 2, P], F32, name="a1_%d" % u, tag="score%d" % (2 + u))
+            for i in range(2):
+                c = 2 * u + i
+                product(a1[:, i, :], keys(slice(c * P, (c + 1) * P)), queries(1))
+            for i in range(2):
+                c = 2 * u + i
+                nc.scalar.activation(z1_turned[:, c, :], a1[:, i, :], ACT.Identity, bias=kb_col[:, c : c + 1])
+        z1 = ps.tile([P, CHUNKS, P], F32, name="z1", tag="kb_turned0")
+        for c in range(CHUNKS):
+            nc.tensor.transpose(z1[:, c, :], z1_turned[:, c, :], ident[:])
+        nc.scalar.activation(y[:, 1, :], z1[:].rearrange("p c n -> p (c n)"), ACT.Sigmoid, bias=neg_th[:, 1:2])
         nc.vector.tensor_copy(map1[:].indirect(offsets[:]), y[:, 1, :])
         nc.sync.dma_start(out[0, P:NQ, :], map1[:])

@@ -43,6 +43,11 @@ def tile_attend_sigscat_topk_kernel(tc, qT, k_words, k_scales, kb, th, offs, out
         half_offsets = [offsets[:, u * (HALF // 16) : (u + 1) * (HALF // 16)] for u in range(2)]
         halves = [slice(u * HALF, (u + 1) * HALF) for u in range(2)]
 
+        warm_in = sb.tile([P, 1], F32, name="warm_in")
+        nc.vector.memset(warm_in[:], 0.0)
+        warm = sb.tile([P, 1], F32, name="warm")
+        nc.scalar.activation(warm[:], warm_in[:], ACT.Sigmoid)
+
         scale_pool = sb.tile([P, T // 4], I32, name="scale_pool")
         nc.gpsimd.memset(scale_pool[:], 0)
         kb_pool = sb.tile([P, T], F32, name="kb_pool")
@@ -69,8 +74,6 @@ def tile_attend_sigscat_topk_kernel(tc, qT, k_words, k_scales, kb, th, offs, out
         map0 = sb.tile([P, T], F32, name="map0")
         nc.gpsimd.memset(kb_pool[0:KB_ROW, KB_SPLIT:T], 0.0)
         nc.gpsimd.memset(map0[:], 0.0)
-        warm = sb.tile([P, 1], F32, name="warm")
-        nc.scalar.activation(warm[:], ident[:, 0:1], ACT.Sigmoid)
 
         kb_listed = sb.tile([P, N], F32, name="kb_listed")
         for u in range(2):

@@ -23,6 +23,7 @@ HALF = N // 2
 CHUNKS = N // P
 KB_ROW = P - 1
 KB_SPLIT = 1472
+WORDS_AHEAD = 768
 
 FLOPS = 2 * NQ * N * D
 BYTES = 4 * D * NQ + D * T + 16 * T + 4 * T + 4 * NQ + 2 * P * (N // 16) + 4 * NQ * T
@@ -58,12 +59,14 @@ def tile_attend_sigscat_topk_kernel(tc, qT, k_words, k_scales, kb, th, offs, out
         q_rows = qT[0].rearrange("(p j) w -> p j w", j=PACK)
         q_raw = [sb.tile([P, PACK, P], F32, name="q_raw%d" % h) for h in range(2)]
         nc.sync.dma_start(q_raw[0][:], q_rows[:, :, 0:P])
+        word_pool = sb.tile([P, T], I32, name="word_pool")
+        words = k_words[0].rearrange("p t r -> p (t r)").bitcast(I32)
+        nc.sync.dma_start(word_pool[:, 0:WORDS_AHEAD], words[:, 0:WORDS_AHEAD])
         for quad in range(4):
             nc.sync.dma_start(
                 scale_pool[32 * quad : 32 * quad + 4, :], k_scales[0, 4 * quad : 4 * quad + 4, :].bitcast(I32)
             )
-        word_pool = sb.tile([P, T], I32, name="word_pool")
-        nc.sync.dma_start(word_pool[:], k_words[0].rearrange("p t r -> p (t r)").bitcast(I32))
+        nc.sync.dma_start(word_pool[:, WORDS_AHEAD:T], words[:, WORDS_AHEAD:T])
         nc.sync.dma_start(q_raw[1][:], q_rows[:, :, P:NQ])
         th_sb = sb.tile([P, 2], F32, name="th_sb")
         with nc.allow_non_contiguous_dma(reason="one threshold a partition for each of the two query tiles"):
@@ -78,8 +81,6 @@ def tile_attend_sigscat_topk_kernel(tc, qT, k_words, k_scales, kb, th, offs, out
         kb_listed = sb.tile([P, N], F32, name="kb_listed")
         for u in range(2):
             nc.vector.tensor_copy(kb_listed[:, halves[u]], kb_pool[:].indirect(half_offsets[u]))
-        k_scale = sb.tile([P, N], U8, name="k_scale", align_bytes=64)
-        nc.vector.tensor_copy(k_scale[:], scale_pool[:].bitcast(U8).indirect(offsets[:]))
 
         kb_col = sb.tile([P, CHUNKS], F32, name="kb_col")
         kb_rows = sb.tile([P, N], F32, name="kb_rows")
@@ -96,7 +97,7 @@ def tile_attend_sigscat_topk_kernel(tc, qT, k_words, k_scales, kb, th, offs, out
             nc.scalar.copy(kb_rows[:, halves[u]], kb_spread[:].rearrange("p c n -> p (c n)"))
 
         q_bf = [
-            sb.tile([P, P, PACK], BF16, name="q_bf0", align_bytes=64),
+            sb.tile([P, P, PACK], BF16, name="q_bf0", tag="k_code", align_bytes=64),
             sb.tile([P, P, PACK], BF16, name="q_bf1", tag="wide1", align_bytes=64),
         ]
         q_code = sb.tile([P, NQ], U32, name="q_code", align_bytes=64)
@@ -112,10 +113,12 @@ def tile_attend_sigscat_topk_kernel(tc, qT, k_words, k_scales, kb, th, offs, out
             )
 
         quantise(0)
+        k_scale = sb.tile([P, N], U8, name="k_scale", align_bytes=64)
+        nc.vector.tensor_copy(k_scale[:], scale_pool[:].bitcast(U8).indirect(offsets[:]))
         neg_th = sb.tile([P, 2], F32, name="neg_th")
         nc.gpsimd.tensor_scalar(neg_th[:], th_sb[:], -1.0, 0.0, ALU.mult, ALU.add)
 
-        k_code = sb.tile([P, N], U32, name="k_code", align_bytes=64)
+        k_code = sb.tile([P, N], U32, name="k_code", tag="k_code", align_bytes=64)
         for u in range(2):
             nc.vector.tensor_copy(k_code[:, halves[u]], word_pool[:].bitcast(U32).indirect(half_offsets[u]))
 

@@ -77,6 +77,8 @@ def tile_attend_sigscat_topk_kernel(tc, qT, k_words, k_scales, kb, th, offs, out
         map0 = sb.tile([P, T], F32, name="map0")
         nc.gpsimd.memset(kb_pool[0:KB_ROW, KB_SPLIT:T], 0.0)
         nc.gpsimd.memset(map0[:], 0.0)
+        zeros = sb.tile([P, P], F32, name="zeros")
+        nc.gpsimd.memset(zeros[:], 0.0)
 
         kb_listed = sb.tile([P, N], F32, name="kb_listed")
         for u in range(2):
@@ -143,20 +145,17 @@ def tile_attend_sigscat_topk_kernel(tc, qT, k_words, k_scales, kb, th, offs, out
             return k_code[:, cols], k_scale[:, cols]
 
         z0 = sb.tile([P, N], F32, name="z0")
-        for u in range(2):
-            a0 = ps.tile([P, HALF], F32, name="a0_%d" % u, tag="score%d" % u)
-            product(a0[:], queries(0), keys(halves[u]))
-            pieces = 2 if u == 0 else 1
-            width = HALF // pieces
-            for i in range(pieces):
-                cols = slice(u * HALF + i * width, u * HALF + (i + 1) * width)
-                nc.vector.tensor_tensor(z0[:, cols], a0[:, i * width : (i + 1) * width], kb_rows[:, cols], ALU.add)
-                nc.scalar.activation(y[:, 0, cols], z0[:, cols], ACT.Sigmoid, bias=neg_th[:, 0:1])
-        quantise(1)
+        for i, cols in enumerate([slice(0, P), slice(P, HALF), halves[1]]):
+            a0 = ps.tile([P, cols.stop - cols.start], F32, name="a0_%d" % i, tag=("score0", "score1", "kb_turned1")[i])
+            product(a0[:], queries(0), keys(cols))
+            nc.vector.tensor_tensor(z0[:, cols], a0[:], kb_rows[:, cols], ALU.add)
+            nc.scalar.activation(y[:, 0, cols], z0[:, cols], ACT.Sigmoid, bias=neg_th[:, 0:1])
+            if i == 1:
+                quantise(1)
         map1 = sb.tile([P, T], F32, name="map1", tag="wide1", align_bytes=64)
         nc.gpsimd.memset(map1[:], 0.0)
-        for u in range(2):
-            nc.vector.tensor_copy(map0[:].indirect(half_offsets[u]), y[:, 0, halves[u]])
+        nc.vector.tensor_tensor(map0[:].indirect(offsets[:, 0 : P // 16]), y[:, 0, 0:P], zeros[:], ALU.add)
+        nc.vector.tensor_copy(map0[:].indirect(offsets[:, P // 16 : N // 16]), y[:, 0, P:N])
         nc.sync.dma_start(out[0, 0:P, :], map0[:])
 
         for u in range(2):

@@ -22,7 +22,7 @@ D = 512
 HALF = N // 2
 CHUNKS = N // P
 KB_ROW = P - 1
-KB_SPLIT = 1472
+KB_SPLIT = 640
 WORDS_AHEAD = 768
 
 FLOPS = 2 * NQ * N * D
@@ -54,6 +54,7 @@ def tile_attend_sigscat_topk_kernel(tc, qT, k_words, k_scales, kb, th, offs, out
         kb_pool = sb.tile([P, T], F32, name="kb_pool")
         for cols in odd_pieces(KB_SPLIT):
             nc.vector.memset(kb_pool[0:KB_ROW, cols].bitcast(I32), 0)
+        nc.vector.memset(kb_pool[0:KB_ROW, KB_SPLIT:T].bitcast(I32), 0)
         nc.sync.dma_start(kb_pool[KB_ROW:P, :], kb[0:1, :])
 
         q_rows = qT[0].rearrange("(p j) w -> p j w", j=PACK)
@@ -75,10 +76,9 @@ def tile_attend_sigscat_topk_kernel(tc, qT, k_words, k_scales, kb, th, offs, out
         ident = sb.tile([P, P], F32, name="ident")
         make_identity(nc, ident[:])
         map0 = sb.tile([P, T], F32, name="map0")
-        nc.gpsimd.memset(kb_pool[0:KB_ROW, KB_SPLIT:T], 0.0)
-        nc.gpsimd.memset(map0[:], 0.0)
         zeros = sb.tile([P, P], F32, name="zeros")
         nc.gpsimd.memset(zeros[:], 0.0)
+        nc.gpsimd.memset(map0[:], 0.0)
 
         kb_listed = sb.tile([P, N], F32, name="kb_listed")
         for u in range(2):

@@ -99,8 +99,8 @@ def tile_attend_sigscat_topk_kernel(tc, qT, k_words, k_scales, kb, th, offs, out
             nc.scalar.copy(kb_rows[:, halves[u]], kb_spread[:].rearrange("p c n -> p (c n)"))
 
         q_bf = [
-            sb.tile([P, P, PACK], BF16, name="q_bf0", tag="k_code", align_bytes=64),
-            sb.tile([P, P, PACK], BF16, name="q_bf1", tag="wide1", align_bytes=64),
+            sb.tile([P, P, PACK], BF16, name="q_bf0", tag="wide1", align_bytes=64),
+            sb.tile([P, P, PACK], BF16, name="q_bf1", align_bytes=64),
         ]
         q_code = sb.tile([P, NQ], U32, name="q_code", align_bytes=64)
         q_scale = sb.tile([P, NQ], U8, name="q_scale", align_bytes=64)
@@ -115,12 +115,14 @@ def tile_attend_sigscat_topk_kernel(tc, qT, k_words, k_scales, kb, th, offs, out
             )
 
         quantise(0)
+        map1 = sb.tile([P, T], F32, name="map1", tag="wide1", align_bytes=64)
+        nc.gpsimd.memset(map1[:], 0.0)
         k_scale = sb.tile([P, N], U8, name="k_scale", align_bytes=64)
         nc.vector.tensor_copy(k_scale[:], scale_pool[:].bitcast(U8).indirect(offsets[:]))
         neg_th = sb.tile([P, 2], F32, name="neg_th")
-        nc.gpsimd.tensor_scalar(neg_th[:], th_sb[:], -1.0, 0.0, ALU.mult, ALU.add)
+        nc.scalar.activation(neg_th[:], th_sb[:], ACT.Copy, scale=-1.0)
 
-        k_code = sb.tile([P, N], U32, name="k_code", tag="k_code", align_bytes=64)
+        k_code = sb.tile([P, N], U32, name="k_code", align_bytes=64)
         for u in range(2):
             nc.vector.tensor_copy(k_code[:, halves[u]], word_pool[:].bitcast(U32).indirect(half_offsets[u]))
 
@@ -152,8 +154,6 @@ def tile_attend_sigscat_topk_kernel(tc, qT, k_words, k_scales, kb, th, offs, out
             nc.scalar.activation(y[:, 0, cols], z0[:, cols], ACT.Sigmoid, bias=neg_th[:, 0:1])
             if i == 1:
                 quantise(1)
-        map1 = sb.tile([P, T], F32, name="map1", tag="wide1", align_bytes=64)
-        nc.gpsimd.memset(map1[:], 0.0)
         nc.vector.tensor_tensor(map0[:].indirect(offsets[:, 0 : P // 16]), y[:, 0, 0:P], zeros[:], ALU.add)
         nc.vector.tensor_copy(map0[:].indirect(offsets[:, P // 16 : N // 16]), y[:, 0, P:N])
         nc.sync.dma_start(out[0, 0:P, :], map0[:])
@@ -166,9 +166,12 @@ def tile_attend_sigscat_topk_kernel(tc, qT, k_words, k_scales, kb, th, offs, out
             for i in range(2):
                 c = 2 * u + i
                 nc.scalar.activation(z1_turned[:, c, :], a1[:, i, :], ACT.Identity, bias=kb_col[:, c : c + 1])
-        z1 = ps.tile([P, CHUNKS, P], F32, name="z1", tag="kb_turned0")
-        for c in range(CHUNKS):
-            nc.tensor.transpose(z1[:, c, :], z1_turned[:, c, :], ident[:])
-        nc.scalar.activation(y[:, 1, :], z1[:].rearrange("p c n -> p (c n)"), ACT.Sigmoid, bias=neg_th[:, 1:2])
+        for u in range(2):
+            z1 = ps.tile([P, 2, P], F32, name="z1_%d" % u, tag=("kb_turned0", "kb_spread0")[u])
+            for i in range(2):
+                nc.tensor.transpose(z1[:, i, :], z1_turned[:, 2 * u + i, :], ident[:])
+            nc.scalar.activation(
+                y[:, 1, halves[u]], z1[:].rearrange("p c n -> p (c n)"), ACT.Sigmoid, bias=neg_th[:, 1:2]
+            )
         nc.vector.tensor_copy(map1[:].indirect(offsets[:]), y[:, 1, :])
         nc.sync.dma_start(out[0, P:NQ, :], map1[:])

@@ -21,9 +21,9 @@ NQ = 256
 D = 512
 HALF = N // 2
 CHUNKS = N // P
+SCALE_ROW = P - 16
 KB_ROW = P - 1
-KB_SPLIT = 640
-WORDS_AHEAD = 768
+KB_SPLIT = 1408
 
 FLOPS = 2 * NQ * N * D
 BYTES = 4 * D * NQ + D * T + 16 * T + 4 * T + 4 * NQ + 2 * P * (N // 16) + 4 * NQ * T
@@ -50,11 +50,11 @@ def tile_attend_sigscat_topk_kernel(tc, qT, k_words, k_scales, kb, th, offs, out
         nc.scalar.activation(warm[:], warm_in[:], ACT.Sigmoid)
 
         scale_pool = sb.tile([P, T // 4], I32, name="scale_pool")
-        nc.gpsimd.memset(scale_pool[:], 0)
+        nc.gpsimd.memset(scale_pool[0:SCALE_ROW, :], 0)
+        nc.sync.dma_start(scale_pool[SCALE_ROW:P, :], k_scales[0].bitcast(I32))
         kb_pool = sb.tile([P, T], F32, name="kb_pool")
         for cols in odd_pieces(KB_SPLIT):
             nc.vector.memset(kb_pool[0:KB_ROW, cols].bitcast(I32), 0)
-        nc.vector.memset(kb_pool[0:KB_ROW, KB_SPLIT:T].bitcast(I32), 0)
         nc.sync.dma_start(kb_pool[KB_ROW:P, :], kb[0:1, :])
 
         q_rows = qT[0].rearrange("(p j) w -> p j w", j=PACK)
@@ -62,12 +62,7 @@ def tile_attend_sigscat_topk_kernel(tc, qT, k_words, k_scales, kb, th, offs, out
         nc.sync.dma_start(q_raw[0][:], q_rows[:, :, 0:P])
         word_pool = sb.tile([P, T], I32, name="word_pool")
         words = k_words[0].rearrange("p t r -> p (t r)").bitcast(I32)
-        nc.sync.dma_start(word_pool[:, 0:WORDS_AHEAD], words[:, 0:WORDS_AHEAD])
-        for quad in range(4):
-            nc.sync.dma_start(
-                scale_pool[32 * quad : 32 * quad + 4, :], k_scales[0, 4 * quad : 4 * quad + 4, :].bitcast(I32)
-            )
-        nc.sync.dma_start(word_pool[:, WORDS_AHEAD:T], words[:, WORDS_AHEAD:T])
+        nc.sync.dma_start(word_pool[:], words)
         nc.sync.dma_start(q_raw[1][:], q_rows[:, :, P:NQ])
         th_sb = sb.tile([P, 2], F32, name="th_sb")
         with nc.allow_non_contiguous_dma(reason="one threshold a partition for each of the two query tiles"):
@@ -75,17 +70,28 @@ def tile_attend_sigscat_topk_kernel(tc, qT, k_words, k_scales, kb, th, offs, out
 
         ident = sb.tile([P, P], F32, name="ident")
         make_identity(nc, ident[:])
+        nc.gpsimd.memset(kb_pool[0:KB_ROW, KB_SPLIT:T].bitcast(I32), 0)
+        k_scale = sb.tile([P, N], U8, name="k_scale", align_bytes=64)
+        nc.gpsimd.memset(k_scale[:].bitcast(I32), 0)
         map0 = sb.tile([P, T], F32, name="map0")
         zeros = sb.tile([P, P], F32, name="zeros")
         nc.gpsimd.memset(zeros[:], 0.0)
         nc.gpsimd.memset(map0[:], 0.0)
+
+        scale_listed = sb.tile([P, N], U8, name="scale_listed")
+        nc.vector.tensor_copy(scale_listed[:], scale_pool[:].bitcast(U8).indirect(offsets[:]))
+        for quad in range(4):
+            first = SCALE_ROW + 4 * quad
+            nc.sync.dma_start(
+                k_scale[32 * quad : 32 * quad + 4, :].bitcast(I32), scale_listed[first : first + 4, :].bitcast(I32)
+            )
 
         kb_listed = sb.tile([P, N], F32, name="kb_listed")
         for u in range(2):
             nc.vector.tensor_copy(kb_listed[:, halves[u]], kb_pool[:].indirect(half_offsets[u]))
 
         kb_col = sb.tile([P, CHUNKS], F32, name="kb_col")
-        kb_rows = sb.tile([P, N], F32, name="kb_rows")
+        kb_rows = [sb.tile([P, HALF], F32, name="kb_rows%d" % u, tag="kb_rows%d" % u, align_bytes=64) for u in range(2)]
         for u in range(2):
             kb_turned = ps.tile([P, 2, P], F32, name="kb_turned%d" % u, tag="kb_turned%d" % u)
             for i in range(2):
@@ -96,36 +102,33 @@ def tile_attend_sigscat_topk_kernel(tc, qT, k_words, k_scales, kb, th, offs, out
             for i in range(2):
                 c = 2 * u + i
                 nc.tensor.transpose(kb_spread[:, i, :], kb_col[:, c : c + 1].to_broadcast([P, P]), ident[:])
-            nc.scalar.copy(kb_rows[:, halves[u]], kb_spread[:].rearrange("p c n -> p (c n)"))
+            nc.scalar.copy(kb_rows[u][:], kb_spread[:].rearrange("p c n -> p (c n)"))
 
         q_bf = [
-            sb.tile([P, P, PACK], BF16, name="q_bf0", tag="wide1", align_bytes=64),
-            sb.tile([P, P, PACK], BF16, name="q_bf1", align_bytes=64),
+            sb.tile([P, P, PACK], BF16, name="q_bf0", align_bytes=64),
+            sb.tile([P, P, PACK], BF16, name="q_bf1", tag="wide1", align_bytes=64),
         ]
-        q_code = sb.tile([P, NQ], U32, name="q_code", align_bytes=64)
         q_scale = sb.tile([P, NQ], U8, name="q_scale", align_bytes=64)
+        q_code = {}
 
-        def quantise(h):
-            rows = slice(h * P, (h + 1) * P)
-            nc.scalar.copy(q_bf[h][:], q_raw[h][:].rearrange("p j w -> p w j"))
+        def quantise(h, tag):
+            q_code[h] = sb.tile([P, P], U32, name="q_code%d" % h, tag=tag, align_bytes=64)
             nc.vector.quantize_mx(
-                out=q_code[:, rows].bitcast(FP8X4),
-                scales=q_scale[:, rows],
+                out=q_code[h][:].bitcast(FP8X4),
+                scales=q_scale[:, h * P : (h + 1) * P],
                 in_=q_bf[h][:].rearrange("p w j -> p (w j)"),
             )
 
-        quantise(0)
-        map1 = sb.tile([P, T], F32, name="map1", tag="wide1", align_bytes=64)
-        nc.gpsimd.memset(map1[:], 0.0)
-        k_scale = sb.tile([P, N], U8, name="k_scale", align_bytes=64)
-        nc.vector.tensor_copy(k_scale[:], scale_pool[:].bitcast(U8).indirect(offsets[:]))
+        nc.scalar.copy(q_bf[0][:], q_raw[0][:].rearrange("p j w -> p w j"))
+        quantise(0, "q_code0")
         neg_th = sb.tile([P, 2], F32, name="neg_th")
-        nc.scalar.activation(neg_th[:], th_sb[:], ACT.Copy, scale=-1.0)
+        nc.gpsimd.tensor_scalar(neg_th[:], th_sb[:], -1.0, 0.0, ALU.mult, ALU.add)
 
         k_code = sb.tile([P, N], U32, name="k_code", align_bytes=64)
         for u in range(2):
             nc.vector.tensor_copy(k_code[:, halves[u]], word_pool[:].bitcast(U32).indirect(half_offsets[u]))
 
+        nc.vector.tensor_copy(q_bf[1][:], q_raw[1][:].rearrange("p j w -> p w j"))
         z1_turned = sb.tile([P, CHUNKS, P], F32, name="z1_turned")
         y = sb.tile([P, 2, N], F32, name="y")
 
@@ -141,7 +144,7 @@ def tile_attend_sigscat_topk_kernel(tc, qT, k_words, k_scales, kb, th, offs, out
             )
 
         def queries(h):
-            return q_code[:, h * P : (h + 1) * P], q_scale[:, h * P : (h + 1) * P]
+            return q_code[h][:], q_scale[:, h * P : (h + 1) * P]
 
         def keys(cols):
             return k_code[:, cols], k_scale[:, cols]
@@ -150,10 +153,12 @@ def tile_attend_sigscat_topk_kernel(tc, qT, k_words, k_scales, kb, th, offs, out
         for i, cols in enumerate([slice(0, P), slice(P, HALF), halves[1]]):
             a0 = ps.tile([P, cols.stop - cols.start], F32, name="a0_%d" % i, tag=("score0", "score1", "kb_turned1")[i])
             product(a0[:], queries(0), keys(cols))
-            nc.vector.tensor_tensor(z0[:, cols], a0[:], kb_rows[:, cols], ALU.add)
+            nc.vector.tensor_tensor(z0[:, cols], a0[:], kb_rows[i // 2][:, cols.start % HALF : (cols.stop - 1) % HALF + 1], ALU.add)
             nc.scalar.activation(y[:, 0, cols], z0[:, cols], ACT.Sigmoid, bias=neg_th[:, 0:1])
             if i == 1:
-                quantise(1)
+                quantise(1, "kb_rows0")
+                map1 = sb.tile([P, T], F32, name="map1", tag="wide1", align_bytes=64)
+                nc.gpsimd.memset(map1[:], 0.0)
         nc.vector.tensor_tensor(map0[:].indirect(offsets[:, 0 : P // 16]), y[:, 0, 0:P], zeros[:], ALU.add)
         nc.vector.tensor_copy(map0[:].indirect(offsets[:, P // 16 : N // 16]), y[:, 0, P:N])
         nc.sync.dma_start(out[0, 0:P, :], map0[:])

@@ -82,7 +82,7 @@ def tile_attend_sigscat_topk_kernel(tc, qT, k_words, k_scales, kb, th, offs, out
         nc.vector.tensor_copy(scale_listed[:], scale_pool[:].bitcast(U8).indirect(offsets[:]))
         for quad in range(4):
             first = SCALE_ROW + 4 * quad
-            nc.sync.dma_start(
+            nc.scalar.dma_start(
                 k_scale[32 * quad : 32 * quad + 4, :].bitcast(I32), scale_listed[first : first + 4, :].bitcast(I32)
             )
 

@@ -76,7 +76,8 @@ def tile_attend_sigscat_topk_kernel(tc, qT, k_words, k_scales, kb, th, offs, out
         map0 = sb.tile([P, T], F32, name="map0")
         zeros = sb.tile([P, P], F32, name="zeros")
         nc.gpsimd.memset(zeros[:], 0.0)
-        nc.gpsimd.memset(map0[:], 0.0)
+        for cols in [slice(0, T // 2)] + [slice(c, c + T // 8) for c in range(T // 2, T, T // 8)]:
+            nc.gpsimd.memset(map0[:, cols], 0.0)
 
         scale_listed = sb.tile([P, N], U8, name="scale_listed")
         nc.vector.tensor_copy(scale_listed[:], scale_pool[:].bitcast(U8).indirect(offsets[:]))
@@ -91,18 +92,20 @@ def tile_attend_sigscat_topk_kernel(tc, qT, k_words, k_scales, kb, th, offs, out
             nc.vector.tensor_copy(kb_listed[:, halves[u]], kb_pool[:].indirect(half_offsets[u]))
 
         kb_col = sb.tile([P, CHUNKS], F32, name="kb_col")
-        kb_rows = [sb.tile([P, HALF], F32, name="kb_rows%d" % u, tag="kb_rows%d" % u, align_bytes=64) for u in range(2)]
-        for u in range(2):
-            kb_turned = ps.tile([P, 2, P], F32, name="kb_turned%d" % u, tag="kb_turned%d" % u)
-            for i in range(2):
-                c = 2 * u + i
-                nc.tensor.transpose(kb_turned[:, i, :], kb_listed[:, c * P : (c + 1) * P], ident[:])
-            nc.scalar.copy(kb_col[:, 2 * u : 2 * u + 2], kb_turned[:, :, KB_ROW])
-            kb_spread = ps.tile([P, 2, P], F32, name="kb_spread%d" % u, tag="kb_spread%d" % u)
-            for i in range(2):
-                c = 2 * u + i
-                nc.tensor.transpose(kb_spread[:, i, :], kb_col[:, c : c + 1].to_broadcast([P, P]), ident[:])
-            nc.scalar.copy(kb_rows[u][:], kb_spread[:].rearrange("p c n -> p (c n)"))
+        pieces = [slice(0, P), slice(P, HALF), halves[1]]
+        kb_rows = []
+        for i, cols in enumerate(pieces):
+            chunks = range(cols.start // P, cols.stop // P)
+            for c in chunks:
+                kb_turned = ps.tile([P, P], F32, name="kb_turned%d" % c, tag="kb_turned%d" % c)
+                nc.tensor.transpose(kb_turned[:], kb_listed[:, c * P : (c + 1) * P], ident[:])
+                nc.scalar.copy(kb_col[:, c : c + 1], kb_turned[:, KB_ROW:P])
+            kb_spread = ps.tile([P, len(chunks), P], F32, name="kb_spread%d" % i, tag="kb_spread%d" % i)
+            for j, c in enumerate(chunks):
+                nc.tensor.transpose(kb_spread[:, j, :], kb_col[:, c : c + 1].to_broadcast([P, P]), ident[:])
+            rows = sb.tile([P, len(chunks) * P], F32, name="kb_rows%d" % i, tag="kb_rows%d" % i, align_bytes=64)
+            nc.scalar.copy(rows[:], kb_spread[:].rearrange("p c n -> p (c n)"))
+            kb_rows.append(rows)
 
         q_bf = [
             sb.tile([P, P, PACK], BF16, name="q_bf0", align_bytes=64),
@@ -121,8 +124,6 @@ def tile_attend_sigscat_topk_kernel(tc, qT, k_words, k_scales, kb, th, offs, out
 
         nc.scalar.copy(q_bf[0][:], q_raw[0][:].rearrange("p j w -> p w j"))
         quantise(0, "q_code0")
-        neg_th = sb.tile([P, 2], F32, name="neg_th")
-        nc.gpsimd.tensor_scalar(neg_th[:], th_sb[:], -1.0, 0.0, ALU.mult, ALU.add)
 
         k_code = sb.tile([P, N], U32, name="k_code", align_bytes=64)
         for u in range(2):
@@ -150,21 +151,25 @@ def tile_attend_sigscat_topk_kernel(tc, qT, k_words, k_scales, kb, th, offs, out
             return k_code[:, cols], k_scale[:, cols]
 
         z0 = sb.tile([P, N], F32, name="z0")
-        for i, cols in enumerate([slice(0, P), slice(P, HALF), halves[1]]):
-            a0 = ps.tile([P, cols.stop - cols.start], F32, name="a0_%d" % i, tag=("score0", "score1", "kb_turned1")[i])
+        for i, cols in enumerate(pieces):
+            a0 = ps.tile([P, cols.stop - cols.start], F32, name="a0_%d" % i, tag=("score0", "kb_turned0", "kb_turned1")[i])
             product(a0[:], queries(0), keys(cols))
-            nc.vector.tensor_tensor(z0[:, cols], a0[:], kb_rows[i // 2][:, cols.start % HALF : (cols.stop - 1) % HALF + 1], ALU.add)
-            nc.scalar.activation(y[:, 0, cols], z0[:, cols], ACT.Sigmoid, bias=neg_th[:, 0:1])
+            nc.vector.scalar_tensor_tensor(
+                out=z0[:, cols], in0=a0[:], scalar=th_sb[:, 0:1], in1=kb_rows[i][:], op0=ALU.subtract, op1=ALU.add
+            )
+            nc.scalar.activation(y[:, 0, cols], z0[:, cols], ACT.Sigmoid)
             if i == 1:
-                quantise(1, "kb_rows0")
+                quantise(1, "kb_rows1")
                 map1 = sb.tile([P, T], F32, name="map1", tag="wide1", align_bytes=64)
                 nc.gpsimd.memset(map1[:], 0.0)
         nc.vector.tensor_tensor(map0[:].indirect(offsets[:, 0 : P // 16]), y[:, 0, 0:P], zeros[:], ALU.add)
         nc.vector.tensor_copy(map0[:].indirect(offsets[:, P // 16 : N // 16]), y[:, 0, P:N])
         nc.sync.dma_start(out[0, 0:P, :], map0[:])
 
+        neg_th = sb.tile([P, 1], F32, name="neg_th", tag="kb_rows2", align_bytes=64)
+        nc.scalar.activation(neg_th[:], th_sb[:, 1:2], ACT.Copy, scale=-1.0)
         for u in range(2):
-            a1 = ps.tile([P, 2, P], F32, name="a1_%d" % u, tag="score%d" % (2 + u))
+            a1 = ps.tile([P, 2, P], F32, name="a1_%d" % u, tag="kb_turned%d" % (2 + u))
             for i in range(2):
                 c = 2 * u + i
                 product(a1[:, i, :], keys(slice(c * P, (c + 1) * P)), queries(1))
@@ -172,11 +177,11 @@ def tile_attend_sigscat_topk_kernel(tc, qT, k_words, k_scales, kb, th, offs, out
                 c = 2 * u + i
                 nc.scalar.activation(z1_turned[:, c, :], a1[:, i, :], ACT.Identity, bias=kb_col[:, c : c + 1])
         for u in range(2):
-            z1 = ps.tile([P, 2, P], F32, name="z1_%d" % u, tag=("kb_turned0", "kb_spread0")[u])
+            z1 = ps.tile([P, 2, P], F32, name="z1_%d" % u, tag="kb_spread%d" % u)
             for i in range(2):
                 nc.tensor.transpose(z1[:, i, :], z1_turned[:, 2 * u + i, :], ident[:])
             nc.scalar.activation(
-                y[:, 1, halves[u]], z1[:].rearrange("p c n -> p (c n)"), ACT.Sigmoid, bias=neg_th[:, 1:2]
+                y[:, 1, halves[u]], z1[:].rearrange("p c n -> p (c n)"), ACT.Sigmoid, bias=neg_th[:]
             )
         nc.vector.tensor_copy(map1[:].indirect(offsets[:]), y[:, 1, :])
         nc.sync.dma_start(out[0, P:NQ, :], map1[:])

@@ -20,6 +20,7 @@ N = 512
 NQ = 256
 D = 512
 HALF = N // 2
+FIRST = 96
 CHUNKS = N // P
 SCALE_ROW = P - 16
 KB_ROW = P - 1
@@ -63,10 +64,10 @@ def tile_attend_sigscat_topk_kernel(tc, qT, k_words, k_scales, kb, th, offs, out
         word_pool = sb.tile([P, T], I32, name="word_pool")
         words = k_words[0].rearrange("p t r -> p (t r)").bitcast(I32)
         nc.sync.dma_start(word_pool[:], words)
-        nc.sync.dma_start(q_raw[1][:], q_rows[:, :, P:NQ])
         th_sb = sb.tile([P, 2], F32, name="th_sb")
         with nc.allow_non_contiguous_dma(reason="one threshold a partition for each of the two query tiles"):
             nc.sync.dma_start(th_sb[:], th[0, :, 0].rearrange("(h p) -> p h", p=P))
+        nc.sync.dma_start(q_raw[1][:], q_rows[:, :, P:NQ])
 
         ident = sb.tile([P, P], F32, name="ident")
         make_identity(nc, ident[:])
@@ -74,7 +75,7 @@ def tile_attend_sigscat_topk_kernel(tc, qT, k_words, k_scales, kb, th, offs, out
         k_scale = sb.tile([P, N], U8, name="k_scale", align_bytes=64)
         nc.gpsimd.memset(k_scale[:].bitcast(I32), 0)
         map0 = sb.tile([P, T], F32, name="map0")
-        zeros = sb.tile([P, P], F32, name="zeros")
+        zeros = sb.tile([P, FIRST], F32, name="zeros")
         nc.gpsimd.memset(zeros[:], 0.0)
         for cols in [slice(0, T // 2)] + [slice(c, c + T // 8) for c in range(T // 2, T, T // 8)]:
             nc.gpsimd.memset(map0[:, cols], 0.0)
@@ -158,30 +159,28 @@ def tile_attend_sigscat_topk_kernel(tc, qT, k_words, k_scales, kb, th, offs, out
                 out=z0[:, cols], in0=a0[:], scalar=th_sb[:, 0:1], in1=kb_rows[i][:], op0=ALU.subtract, op1=ALU.add
             )
             nc.scalar.activation(y[:, 0, cols], z0[:, cols], ACT.Sigmoid)
-            if i == 1:
-                quantise(1, "kb_rows1")
-                map1 = sb.tile([P, T], F32, name="map1", tag="wide1", align_bytes=64)
-                nc.gpsimd.memset(map1[:], 0.0)
-        nc.vector.tensor_tensor(map0[:].indirect(offsets[:, 0 : P // 16]), y[:, 0, 0:P], zeros[:], ALU.add)
-        nc.vector.tensor_copy(map0[:].indirect(offsets[:, P // 16 : N // 16]), y[:, 0, P:N])
+        nc.vector.tensor_tensor(map0[:].indirect(offsets[:, 0 : FIRST // 16]), y[:, 0, 0:FIRST], zeros[:], ALU.add)
+        quantise(1, "kb_rows2")
+        map1 = sb.tile([P, T], F32, name="map1", tag="wide1", align_bytes=64)
+        nc.gpsimd.memset(map1[:], 0.0)
+        nc.vector.tensor_copy(map0[:].indirect(offsets[:, FIRST // 16 : N // 16]), y[:, 0, FIRST:N])
         nc.sync.dma_start(out[0, 0:P, :], map0[:])
 
-        neg_th = sb.tile([P, 1], F32, name="neg_th", tag="kb_rows2", align_bytes=64)
+        neg_th = sb.tile([P, 1], F32, name="neg_th", tag="kb_rows1", align_bytes=64)
         nc.scalar.activation(neg_th[:], th_sb[:, 1:2], ACT.Copy, scale=-1.0)
-        for u in range(2):
-            a1 = ps.tile([P, 2, P], F32, name="a1_%d" % u, tag="kb_turned%d" % (2 + u))
-            for i in range(2):
-                c = 2 * u + i
-                product(a1[:, i, :], keys(slice(c * P, (c + 1) * P)), queries(1))
-            for i in range(2):
-                c = 2 * u + i
-                nc.scalar.activation(z1_turned[:, c, :], a1[:, i, :], ACT.Identity, bias=kb_col[:, c : c + 1])
-        for u in range(2):
-            z1 = ps.tile([P, 2, P], F32, name="z1_%d" % u, tag="kb_spread%d" % u)
-            for i in range(2):
-                nc.tensor.transpose(z1[:, i, :], z1_turned[:, 2 * u + i, :], ident[:])
+        for c in range(CHUNKS):
+            a1 = ps.tile([P, P], F32, name="a1_%d" % c, tag="kb_turned%d" % ((c + 2) % CHUNKS))
+            product(a1[:], keys(slice(c * P, (c + 1) * P)), queries(1))
+            nc.scalar.activation(z1_turned[:, c, :], a1[:], ACT.Identity, bias=kb_col[:, c : c + 1])
+        for i, chunks in enumerate([range(0, 2), range(2, 3), range(3, 4)]):
+            z1 = ps.tile([P, len(chunks), P], F32, name="z1_%d" % i, tag="kb_spread%d" % i)
+            for j, c in enumerate(chunks):
+                nc.tensor.transpose(z1[:, j, :], z1_turned[:, c, :], ident[:])
             nc.scalar.activation(
-                y[:, 1, halves[u]], z1[:].rearrange("p c n -> p (c n)"), ACT.Sigmoid, bias=neg_th[:]
+                y[:, 1, chunks.start * P : chunks.stop * P],
+                z1[:].rearrange("p c n -> p (c n)"),
+                ACT.Sigmoid,
+                bias=neg_th[:],
             )
         nc.vector.tensor_copy(map1[:].indirect(offsets[:]), y[:, 1, :])
         nc.sync.dma_start(out[0, P:NQ, :], map1[:])

@@ -61,7 +61,7 @@ def tile_attend_sigscat_topk_kernel(tc, qT, k_words, k_scales, kb, th, offs, out
         q_rows = qT[0].rearrange("(p j) w -> p j w", j=PACK)
         q_raw = [sb.tile([P, PACK, P], F32, name="q_raw%d" % h) for h in range(2)]
         nc.sync.dma_start(q_raw[0][:], q_rows[:, :, 0:P])
-        word_pool = sb.tile([P, T], I32, name="word_pool")
+        word_pool = sb.tile([P, T], I32, name="word_pool", tag="wide1", align_bytes=64)
         words = k_words[0].rearrange("p t r -> p (t r)").bitcast(I32)
         nc.sync.dma_start(word_pool[:], words)
         th_sb = sb.tile([P, 2], F32, name="th_sb")
@@ -108,10 +108,7 @@ def tile_attend_sigscat_topk_kernel(tc, qT, k_words, k_scales, kb, th, offs, out
             nc.scalar.copy(rows[:], kb_spread[:].rearrange("p c n -> p (c n)"))
             kb_rows.append(rows)
 
-        q_bf = [
-            sb.tile([P, P, PACK], BF16, name="q_bf0", align_bytes=64),
-            sb.tile([P, P, PACK], BF16, name="q_bf1", tag="wide1", align_bytes=64),
-        ]
+        q_bf = [sb.tile([P, P, PACK], BF16, name="q_bf0", align_bytes=64)]
         q_scale = sb.tile([P, NQ], U8, name="q_scale", align_bytes=64)
         q_code = {}
 
@@ -130,7 +127,8 @@ def tile_attend_sigscat_topk_kernel(tc, qT, k_words, k_scales, kb, th, offs, out
         for u in range(2):
             nc.vector.tensor_copy(k_code[:, halves[u]], word_pool[:].bitcast(U32).indirect(half_offsets[u]))
 
-        nc.vector.tensor_copy(q_bf[1][:], q_raw[1][:].rearrange("p j w -> p w j"))
+        q_bf.append(sb.tile([P, P, PACK], BF16, name="q_bf1", tag="wide1", align_bytes=64))
+        nc.gpsimd.tensor_scalar(q_bf[1][:], q_raw[1][:].rearrange("p j w -> p w j"), 1.0, 0.0, ALU.mult, ALU.add)
         z1_turned = sb.tile([P, CHUNKS, P], F32, name="z1_turned")
         y = sb.tile([P, 2, N], F32, name="y")
 

@@ -20,7 +20,6 @@ N = 512
 NQ = 256
 D = 512
 HALF = N // 2
-FIRST = 96
 CHUNKS = N // P
 SCALE_ROW = P - 16
 KB_ROW = P - 1
@@ -38,47 +37,59 @@ def tile_attend_sigscat_topk_kernel(tc, qT, k_words, k_scales, kb, th, offs, out
     nc = tc.nc
     with ExitStack() as ctx:
         sb = ctx.enter_context(tc.tile_pool(name="sb", bufs=1))
+        shared = ctx.enter_context(tc.tile_pool(name="shared", bufs=1))
         ps = ctx.enter_context(tc.psum_pool(name="ps", bufs=1))
+
+        def bank(b, name, width):
+            return ps.tile([P, width], F32, name=name, tag="bank%d" % b)
 
         offsets = sb.tile([P, N // 16], U16, name="offsets")
         nc.sync.dma_start(offsets[:], offs)
-        half_offsets = [offsets[:, u * (HALF // 16) : (u + 1) * (HALF // 16)] for u in range(2)]
+
+        def listed(window, cols):
+            return window.indirect(offsets[:, cols.start // 16 : cols.stop // 16])
+
         halves = [slice(u * HALF, (u + 1) * HALF) for u in range(2)]
+        chunk = [slice(c * P, (c + 1) * P) for c in range(CHUNKS)]
 
         warm_in = sb.tile([P, 1], F32, name="warm_in")
         nc.vector.memset(warm_in[:], 0.0)
         warm = sb.tile([P, 1], F32, name="warm")
         nc.scalar.activation(warm[:], warm_in[:], ACT.Sigmoid)
 
-        scale_pool = sb.tile([P, T // 4], I32, name="scale_pool")
+        ident = sb.tile([P, P], F32, name="ident")
+        make_identity(nc, ident[:])
+        scale_pool = sb.tile([P, T // 4], I32, name="scale_pool", tag="scale_pool")
         nc.gpsimd.memset(scale_pool[0:SCALE_ROW, :], 0)
         nc.sync.dma_start(scale_pool[SCALE_ROW:P, :], k_scales[0].bitcast(I32))
-        kb_pool = sb.tile([P, T], F32, name="kb_pool")
+        k_scale = sb.tile([P, N], U8, name="k_scale", align_bytes=64)
+        nc.gpsimd.memset(k_scale[:].bitcast(I32), 0)
+        kb_pool = shared.tile([P, T], F32, name="kb_pool", offset=0, align_bytes=64)
         for cols in odd_pieces(KB_SPLIT):
             nc.vector.memset(kb_pool[0:KB_ROW, cols].bitcast(I32), 0)
         nc.sync.dma_start(kb_pool[KB_ROW:P, :], kb[0:1, :])
 
         q_rows = qT[0].rearrange("(p j) w -> p j w", j=PACK)
-        q_raw = [sb.tile([P, PACK, P], F32, name="q_raw%d" % h) for h in range(2)]
-        nc.sync.dma_start(q_raw[0][:], q_rows[:, :, 0:P])
-        word_pool = sb.tile([P, T], I32, name="word_pool", tag="wide1", align_bytes=64)
+        q_raw0 = sb.tile([P, PACK, P], F32, name="q_raw0")
+        nc.sync.dma_start(q_raw0[:], q_rows[:, :, 0:P])
+        th_rows = sb.tile([P, P], F32, name="th_rows")
+        nc.sync.dma_start(th_rows[P - 2 : P, :], th[0].rearrange("(h p) o -> h (p o)", h=2))
+        word_pool = sb.tile([P, T], I32, name="word_pool")
         words = k_words[0].rearrange("p t r -> p (t r)").bitcast(I32)
         nc.sync.dma_start(word_pool[:], words)
-        th_sb = sb.tile([P, 2], F32, name="th_sb")
-        with nc.allow_non_contiguous_dma(reason="one threshold a partition for each of the two query tiles"):
-            nc.sync.dma_start(th_sb[:], th[0, :, 0].rearrange("(h p) -> p h", p=P))
-        nc.sync.dma_start(q_raw[1][:], q_rows[:, :, P:NQ])
+        q_raw1 = sb.tile([P, PACK, P], F32, name="q_raw1")
+        nc.sync.dma_start(q_raw1[:], q_rows[:, :, P:NQ])
 
-        ident = sb.tile([P, P], F32, name="ident")
-        make_identity(nc, ident[:])
         nc.gpsimd.memset(kb_pool[0:KB_ROW, KB_SPLIT:T].bitcast(I32), 0)
-        k_scale = sb.tile([P, N], U8, name="k_scale", align_bytes=64)
-        nc.gpsimd.memset(k_scale[:].bitcast(I32), 0)
+        nc.gpsimd.memset(th_rows[0 : P - 2, :], 0.0)
         map0 = sb.tile([P, T], F32, name="map0")
-        zeros = sb.tile([P, FIRST], F32, name="zeros")
-        nc.gpsimd.memset(zeros[:], 0.0)
         for cols in [slice(0, T // 2)] + [slice(c, c + T // 8) for c in range(T // 2, T, T // 8)]:
             nc.gpsimd.memset(map0[:, cols], 0.0)
+
+        th_turned = bank(4, "th_turned", P)
+        nc.tensor.transpose(th_turned[:], th_rows[:], ident[:])
+        neg_th = sb.tile([P, 2], F32, name="neg_th")
+        nc.scalar.activation(neg_th[:], th_turned[:, P - 2 : P], ACT.Copy, scale=-1.0)
 
         scale_listed = sb.tile([P, N], U8, name="scale_listed")
         nc.vector.tensor_copy(scale_listed[:], scale_pool[:].bitcast(U8).indirect(offsets[:]))
@@ -88,48 +99,52 @@ def tile_attend_sigscat_topk_kernel(tc, qT, k_words, k_scales, kb, th, offs, out
                 k_scale[32 * quad : 32 * quad + 4, :].bitcast(I32), scale_listed[first : first + 4, :].bitcast(I32)
             )
 
-        kb_listed = sb.tile([P, N], F32, name="kb_listed")
+        kb_listed = shared.tile([P, N], F32, name="kb_listed", offset=4 * T, align_bytes=64)
         for u in range(2):
-            nc.vector.tensor_copy(kb_listed[:, halves[u]], kb_pool[:].indirect(half_offsets[u]))
+            nc.vector.tensor_copy(kb_listed[:, halves[u]], listed(kb_pool[:], halves[u]))
 
         kb_col = sb.tile([P, CHUNKS], F32, name="kb_col")
-        pieces = [slice(0, P), slice(P, HALF), halves[1]]
-        kb_rows = []
-        for i, cols in enumerate(pieces):
-            chunks = range(cols.start // P, cols.stop // P)
-            for c in chunks:
-                kb_turned = ps.tile([P, P], F32, name="kb_turned%d" % c, tag="kb_turned%d" % c)
-                nc.tensor.transpose(kb_turned[:], kb_listed[:, c * P : (c + 1) * P], ident[:])
-                nc.scalar.copy(kb_col[:, c : c + 1], kb_turned[:, KB_ROW:P])
-            kb_spread = ps.tile([P, len(chunks), P], F32, name="kb_spread%d" % i, tag="kb_spread%d" % i)
-            for j, c in enumerate(chunks):
-                nc.tensor.transpose(kb_spread[:, j, :], kb_col[:, c : c + 1].to_broadcast([P, P]), ident[:])
-            rows = sb.tile([P, len(chunks) * P], F32, name="kb_rows%d" % i, tag="kb_rows%d" % i, align_bytes=64)
-            nc.scalar.copy(rows[:], kb_spread[:].rearrange("p c n -> p (c n)"))
-            kb_rows.append(rows)
+        late = 4 * T + 4 * N
 
-        q_bf = [sb.tile([P, P, PACK], BF16, name="q_bf0", align_bytes=64)]
+        def turn_kb(u):
+            turned = bank(0, "kb_turned%d" % u, HALF)
+            for c in range(2):
+                nc.tensor.transpose(turned[:, chunk[c]], kb_listed[:, chunk[2 * u + c]], ident[:])
+            nc.scalar.copy(kb_col[:, 2 * u : 2 * u + 2], turned[:].rearrange("p (c n) -> p c n", n=P)[:, :, KB_ROW])
+
+        turn_kb(0)
+        kb_rows = []
+        for c in range(2):
+            kb_spread = bank(2 + c, "kb_spread%d" % c, P)
+            nc.tensor.transpose(kb_spread[:], kb_col[:, c : c + 1].to_broadcast([P, P]), ident[:])
+            rows = shared.tile([P, P], F32, name="kb_rows%d" % c, offset=late + (1920, 0)[c], align_bytes=64)
+            nc.scalar.copy(rows[:], kb_spread[:])
+            kb_rows.append(rows)
+        turn_kb(1)
+
         q_scale = sb.tile([P, NQ], U8, name="q_scale", align_bytes=64)
         q_code = {}
 
-        def quantise(h, tag):
-            q_code[h] = sb.tile([P, P], U32, name="q_code%d" % h, tag=tag, align_bytes=64)
+        def quantise(h, codes, q_bf):
+            q_code[h] = codes
             nc.vector.quantize_mx(
-                out=q_code[h][:].bitcast(FP8X4),
-                scales=q_scale[:, h * P : (h + 1) * P],
-                in_=q_bf[h][:].rearrange("p w j -> p (w j)"),
+                out=codes[:].bitcast(FP8X4),
+                scales=q_scale[:, chunk[h]],
+                in_=q_bf[:].rearrange("p w j -> p (w j)"),
             )
 
-        nc.scalar.copy(q_bf[0][:], q_raw[0][:].rearrange("p j w -> p w j"))
-        quantise(0, "q_code0")
+        q_bf0 = sb.tile([P, P, PACK], BF16, name="q_bf0", tag="wide", align_bytes=64)
+        nc.scalar.copy(q_bf0[:], q_raw0[:].rearrange("p j w -> p w j"))
+        quantise(0, shared.tile([P, P], U32, name="q_code0", offset=0, align_bytes=64), q_bf0)
+        map1 = sb.tile([P, T], F32, name="map1", tag="wide", align_bytes=64)
+        nc.gpsimd.memset(map1[:, 0 : T // 2], 0.0)
 
-        k_code = sb.tile([P, N], U32, name="k_code", align_bytes=64)
+        k_code = shared.tile([P, N], U32, name="k_code", offset=4 * P, align_bytes=64)
         for u in range(2):
-            nc.vector.tensor_copy(k_code[:, halves[u]], word_pool[:].bitcast(U32).indirect(half_offsets[u]))
+            nc.vector.tensor_copy(k_code[:, halves[u]], listed(word_pool[:].bitcast(U32), halves[u]))
 
-        q_bf.append(sb.tile([P, P, PACK], BF16, name="q_bf1", tag="wide1", align_bytes=64))
-        nc.gpsimd.tensor_scalar(q_bf[1][:], q_raw[1][:].rearrange("p j w -> p w j"), 1.0, 0.0, ALU.mult, ALU.add)
-        z1_turned = sb.tile([P, CHUNKS, P], F32, name="z1_turned")
+        q_bf1 = shared.tile([P, P, PACK], BF16, name="q_bf1", offset=4 * T - 1024, align_bytes=64)
+        nc.vector.tensor_copy(q_bf1[:], q_raw1[:].rearrange("p j w -> p w j"))
         y = sb.tile([P, 2, N], F32, name="y")
 
         def product(dst, stationary, moving):
@@ -144,41 +159,40 @@ def tile_attend_sigscat_topk_kernel(tc, qT, k_words, k_scales, kb, th, offs, out
             )
 
         def queries(h):
-            return q_code[h][:], q_scale[:, h * P : (h + 1) * P]
+            return q_code[h][:], q_scale[:, chunk[h]]
 
         def keys(cols):
             return k_code[:, cols], k_scale[:, cols]
 
-        z0 = sb.tile([P, N], F32, name="z0")
-        for i, cols in enumerate(pieces):
-            a0 = ps.tile([P, cols.stop - cols.start], F32, name="a0_%d" % i, tag=("score0", "kb_turned0", "kb_turned1")[i])
-            product(a0[:], queries(0), keys(cols))
-            nc.vector.scalar_tensor_tensor(
-                out=z0[:, cols], in0=a0[:], scalar=th_sb[:, 0:1], in1=kb_rows[i][:], op0=ALU.subtract, op1=ALU.add
-            )
-            nc.scalar.activation(y[:, 0, cols], z0[:, cols], ACT.Sigmoid)
-        nc.vector.tensor_tensor(map0[:].indirect(offsets[:, 0 : FIRST // 16]), y[:, 0, 0:FIRST], zeros[:], ALU.add)
-        quantise(1, "kb_rows2")
-        map1 = sb.tile([P, T], F32, name="map1", tag="wide1", align_bytes=64)
-        nc.gpsimd.memset(map1[:], 0.0)
-        nc.vector.tensor_copy(map0[:].indirect(offsets[:, FIRST // 16 : N // 16]), y[:, 0, FIRST:N])
-        nc.sync.dma_start(out[0, 0:P, :], map0[:])
+        for c in range(2):
+            a = bank(4 + c, "a0_%d" % c, P)
+            product(a[:], queries(0), keys(chunk[c]))
+            z = shared.tile([P, P], F32, name="z0_%d" % c, offset=late + (2560, 512)[c], align_bytes=64)
+            nc.vector.tensor_tensor(z[:], a[:], kb_rows[c][:], ALU.add)
+            nc.scalar.activation(y[:, 0, chunk[c]], z[:], ACT.Sigmoid, bias=neg_th[:, 0:1])
+        quantise(1, shared.tile([P, P], U32, name="q_code1", offset=late + 2048, align_bytes=64), q_bf1)
+        zeros = shared.tile([P, P], F32, name="zeros", offset=4 * T - 1024, align_bytes=64)
+        nc.gpsimd.memset(zeros[:], 0.0)
+        nc.gpsimd.memset(map1[:, T // 2 : T], 0.0)
+        nc.vector.tensor_copy(listed(map0[:], halves[0]), y[:, 0, halves[0]])
 
-        neg_th = sb.tile([P, 1], F32, name="neg_th", tag="kb_rows1", align_bytes=64)
-        nc.scalar.activation(neg_th[:], th_sb[:, 1:2], ACT.Copy, scale=-1.0)
-        for c in range(CHUNKS):
-            a1 = ps.tile([P, P], F32, name="a1_%d" % c, tag="kb_turned%d" % ((c + 2) % CHUNKS))
-            product(a1[:], keys(slice(c * P, (c + 1) * P)), queries(1))
-            nc.scalar.activation(z1_turned[:, c, :], a1[:], ACT.Identity, bias=kb_col[:, c : c + 1])
-        for i, chunks in enumerate([range(0, 2), range(2, 3), range(3, 4)]):
-            z1 = ps.tile([P, len(chunks), P], F32, name="z1_%d" % i, tag="kb_spread%d" % i)
+        def long_road(h, chunks, score_banks, turn_bank, turned):
             for j, c in enumerate(chunks):
-                nc.tensor.transpose(z1[:, j, :], z1_turned[:, c, :], ident[:])
-            nc.scalar.activation(
-                y[:, 1, chunks.start * P : chunks.stop * P],
-                z1[:].rearrange("p c n -> p (c n)"),
-                ACT.Sigmoid,
-                bias=neg_th[:],
-            )
-        nc.vector.tensor_copy(map1[:].indirect(offsets[:]), y[:, 1, :])
+                a = bank(score_banks[j], "a%d_%d" % (h, c), P)
+                product(a[:], keys(chunk[c]), queries(h))
+                nc.scalar.activation(turned[:, j, :], a[:], ACT.Identity, bias=kb_col[:, c : c + 1])
+            z = bank(turn_bank, "z%d_%d" % (h, chunks.start), len(chunks) * P)
+            for j, c in enumerate(chunks):
+                nc.tensor.transpose(z[:, chunk[j]], turned[:, j, :], ident[:])
+            cols = slice(chunks.start * P, chunks.stop * P)
+            nc.scalar.activation(y[:, h, cols], z[:], ACT.Sigmoid, bias=neg_th[:, h : h + 1])
+            return cols
+
+        cols = long_road(1, range(0, 1), [2], 6, shared.tile([P, 1, P], F32, name="turned1a", offset=late + 256, align_bytes=64))
+        nc.vector.tensor_tensor(listed(map1[:], cols), y[:, 1, cols], zeros[:], ALU.add)
+        cols = long_road(0, range(2, 4), [0, 1], 2, shared.tile([P, 2, P], F32, name="turned0", offset=late + 2816, align_bytes=64))
+        nc.vector.tensor_copy(listed(map0[:], cols), y[:, 0, cols])
+        nc.sync.dma_start(out[0, 0:P, :], map0[:])
+        cols = long_road(1, range(1, 4), [3, 4, 5], 0, shared.tile([P, 3, P], F32, name="turned1b", offset=late + 3328, align_bytes=64))
+        nc.vector.tensor_copy(listed(map1[:], cols), y[:, 1, cols])
         nc.sync.dma_start(out[0, P:NQ, :], map1[:])

@@ -20,6 +20,7 @@ N = 512
 NQ = 256
 D = 512
 HALF = N // 2
+FILL = 64
 CHUNKS = N // P
 SCALE_ROW = P - 16
 KB_ROW = P - 1
@@ -57,13 +58,9 @@ def tile_attend_sigscat_topk_kernel(tc, qT, k_words, k_scales, kb, th, offs, out
         warm = sb.tile([P, 1], F32, name="warm")
         nc.scalar.activation(warm[:], warm_in[:], ACT.Sigmoid)
 
-        ident = sb.tile([P, P], F32, name="ident")
-        make_identity(nc, ident[:])
         scale_pool = sb.tile([P, T // 4], I32, name="scale_pool", tag="scale_pool")
         nc.gpsimd.memset(scale_pool[0:SCALE_ROW, :], 0)
         nc.sync.dma_start(scale_pool[SCALE_ROW:P, :], k_scales[0].bitcast(I32))
-        k_scale = sb.tile([P, N], U8, name="k_scale", align_bytes=64)
-        nc.gpsimd.memset(k_scale[:].bitcast(I32), 0)
         kb_pool = shared.tile([P, T], F32, name="kb_pool", offset=0, align_bytes=64)
         for cols in odd_pieces(KB_SPLIT):
             nc.vector.memset(kb_pool[0:KB_ROW, cols].bitcast(I32), 0)
@@ -80,8 +77,12 @@ def tile_attend_sigscat_topk_kernel(tc, qT, k_words, k_scales, kb, th, offs, out
         q_raw1 = sb.tile([P, PACK, P], F32, name="q_raw1")
         nc.sync.dma_start(q_raw1[:], q_rows[:, :, P:NQ])
 
-        nc.gpsimd.memset(kb_pool[0:KB_ROW, KB_SPLIT:T].bitcast(I32), 0)
+        ident = sb.tile([P, P], F32, name="ident")
+        make_identity(nc, ident[:])
         nc.gpsimd.memset(th_rows[0 : P - 2, :], 0.0)
+        k_scale = sb.tile([P, N], U8, name="k_scale", align_bytes=64)
+        nc.gpsimd.memset(k_scale[:].bitcast(I32), 0)
+        nc.gpsimd.memset(kb_pool[0:KB_ROW, KB_SPLIT:T].bitcast(I32), 0)
         map0 = sb.tile([P, T], F32, name="map0")
         for cols in [slice(0, T // 2)] + [slice(c, c + T // 8) for c in range(T // 2, T, T // 8)]:
             nc.gpsimd.memset(map0[:, cols], 0.0)
@@ -137,7 +138,8 @@ def tile_attend_sigscat_topk_kernel(tc, qT, k_words, k_scales, kb, th, offs, out
         nc.scalar.copy(q_bf0[:], q_raw0[:].rearrange("p j w -> p w j"))
         quantise(0, shared.tile([P, P], U32, name="q_code0", offset=0, align_bytes=64), q_bf0)
         map1 = sb.tile([P, T], F32, name="map1", tag="wide", align_bytes=64)
-        nc.gpsimd.memset(map1[:, 0 : T // 2], 0.0)
+        for cols in [slice(0, 7 * P)] + [slice(c, c + P) for c in range(7 * P, T, P)]:
+            nc.gpsimd.memset(map1[:, cols], 0.0)
 
         k_code = shared.tile([P, N], U32, name="k_code", offset=4 * P, align_bytes=64)
         for u in range(2):
@@ -171,9 +173,8 @@ def tile_attend_sigscat_topk_kernel(tc, qT, k_words, k_scales, kb, th, offs, out
             nc.vector.tensor_tensor(z[:], a[:], kb_rows[c][:], ALU.add)
             nc.scalar.activation(y[:, 0, chunk[c]], z[:], ACT.Sigmoid, bias=neg_th[:, 0:1])
         quantise(1, shared.tile([P, P], U32, name="q_code1", offset=late + 2048, align_bytes=64), q_bf1)
-        zeros = shared.tile([P, P], F32, name="zeros", offset=4 * T - 1024, align_bytes=64)
+        zeros = shared.tile([P, FILL], F32, name="zeros", offset=4 * T - 1024, align_bytes=64)
         nc.gpsimd.memset(zeros[:], 0.0)
-        nc.gpsimd.memset(map1[:, T // 2 : T], 0.0)
         nc.vector.tensor_copy(listed(map0[:], halves[0]), y[:, 0, halves[0]])
 
         def long_road(h, chunks, score_banks, turn_bank, turned):
@@ -189,10 +190,12 @@ def tile_attend_sigscat_topk_kernel(tc, qT, k_words, k_scales, kb, th, offs, out
             return cols
 
         cols = long_road(1, range(0, 1), [2], 6, shared.tile([P, 1, P], F32, name="turned1a", offset=late + 256, align_bytes=64))
+        cols = slice(0, FILL)
         nc.vector.tensor_tensor(listed(map1[:], cols), y[:, 1, cols], zeros[:], ALU.add)
         cols = long_road(0, range(2, 4), [0, 1], 2, shared.tile([P, 2, P], F32, name="turned0", offset=late + 2816, align_bytes=64))
         nc.vector.tensor_copy(listed(map0[:], cols), y[:, 0, cols])
         nc.sync.dma_start(out[0, 0:P, :], map0[:])
         cols = long_road(1, range(1, 4), [3, 4, 5], 0, shared.tile([P, 3, P], F32, name="turned1b", offset=late + 3328, align_bytes=64))
+        cols = slice(FILL, N)
         nc.vector.tensor_copy(listed(map1[:], cols), y[:, 1, cols])
         nc.sync.dma_start(out[0, P:NQ, :], map1[:])

@@ -20,11 +20,12 @@ N = 512
 NQ = 256
 D = 512
 HALF = N // 2
-FILL = 64
+MAP1_EARLY = 384
+FILL = 96
 CHUNKS = N // P
 SCALE_ROW = P - 16
 KB_ROW = P - 1
-KB_SPLIT = 1408
+KB_SPLIT = 1664
 
 FLOPS = 2 * NQ * N * D
 BYTES = 4 * D * NQ + D * T + 16 * T + 4 * T + 4 * NQ + 2 * P * (N // 16) + 4 * NQ * T
@@ -74,7 +75,8 @@ def tile_attend_sigscat_topk_kernel(tc, qT, k_words, k_scales, kb, th, offs, out
         word_pool = sb.tile([P, T], I32, name="word_pool")
         words = k_words[0].rearrange("p t r -> p (t r)").bitcast(I32)
         nc.sync.dma_start(word_pool[:], words)
-        q_raw1 = sb.tile([P, PACK, P], F32, name="q_raw1")
+        raw1 = 12 * T
+        q_raw1 = shared.tile([P, PACK, P], F32, name="q_raw1", offset=raw1, align_bytes=64)
         nc.sync.dma_start(q_raw1[:], q_rows[:, :, P:NQ])
 
         ident = sb.tile([P, P], F32, name="ident")
@@ -84,8 +86,9 @@ def tile_attend_sigscat_topk_kernel(tc, qT, k_words, k_scales, kb, th, offs, out
         nc.gpsimd.memset(k_scale[:].bitcast(I32), 0)
         nc.gpsimd.memset(kb_pool[0:KB_ROW, KB_SPLIT:T].bitcast(I32), 0)
         map0 = sb.tile([P, T], F32, name="map0")
-        for cols in [slice(0, T // 2)] + [slice(c, c + T // 8) for c in range(T // 2, T, T // 8)]:
-            nc.gpsimd.memset(map0[:, cols], 0.0)
+        nc.gpsimd.memset(map0[:], 0.0)
+        map1 = sb.tile([P, T], F32, name="map1")
+        nc.gpsimd.memset(map1[:, 0:MAP1_EARLY], 0.0)
 
         th_turned = bank(4, "th_turned", P)
         nc.tensor.transpose(th_turned[:], th_rows[:], ident[:])
@@ -107,17 +110,21 @@ def tile_attend_sigscat_topk_kernel(tc, qT, k_words, k_scales, kb, th, offs, out
         kb_col = sb.tile([P, CHUNKS], F32, name="kb_col")
         late = 4 * T + 4 * N
 
+        kb_first = shared.tile([P, 1], F32, name="kb_first", offset=14 * T, align_bytes=64)
+
         def turn_kb(u):
             turned = bank(0, "kb_turned%d" % u, HALF)
             for c in range(2):
                 nc.tensor.transpose(turned[:, chunk[c]], kb_listed[:, chunk[2 * u + c]], ident[:])
+            if u == 0:
+                nc.scalar.copy(kb_first[:], turned[:, KB_ROW:P])
             nc.scalar.copy(kb_col[:, 2 * u : 2 * u + 2], turned[:].rearrange("p (c n) -> p c n", n=P)[:, :, KB_ROW])
 
         turn_kb(0)
         kb_rows = []
         for c in range(2):
             kb_spread = bank(2 + c, "kb_spread%d" % c, P)
-            nc.tensor.transpose(kb_spread[:], kb_col[:, c : c + 1].to_broadcast([P, P]), ident[:])
+            nc.tensor.transpose(kb_spread[:], (kb_first[:], kb_col[:, 1:2])[c].to_broadcast([P, P]), ident[:])
             rows = shared.tile([P, P], F32, name="kb_rows%d" % c, offset=late + (1920, 0)[c], align_bytes=64)
             nc.scalar.copy(rows[:], kb_spread[:])
             kb_rows.append(rows)
@@ -137,17 +144,17 @@ def tile_attend_sigscat_topk_kernel(tc, qT, k_words, k_scales, kb, th, offs, out
         q_bf0 = sb.tile([P, P, PACK], BF16, name="q_bf0", tag="wide", align_bytes=64)
         nc.scalar.copy(q_bf0[:], q_raw0[:].rearrange("p j w -> p w j"))
         quantise(0, shared.tile([P, P], U32, name="q_code0", offset=0, align_bytes=64), q_bf0)
-        map1 = sb.tile([P, T], F32, name="map1", tag="wide", align_bytes=64)
-        for cols in [slice(0, 7 * P)] + [slice(c, c + P) for c in range(7 * P, T, P)]:
-            nc.gpsimd.memset(map1[:, cols], 0.0)
+        zeros = sb.tile([P, FILL], F32, name="zeros", tag="wide", align_bytes=64)
+        nc.gpsimd.memset(zeros[:], 0.0)
+        nc.gpsimd.memset(map1[:, MAP1_EARLY:T], 0.0)
 
         k_code = shared.tile([P, N], U32, name="k_code", offset=4 * P, align_bytes=64)
         for u in range(2):
             nc.vector.tensor_copy(k_code[:, halves[u]], listed(word_pool[:].bitcast(U32), halves[u]))
 
-        q_bf1 = shared.tile([P, P, PACK], BF16, name="q_bf1", offset=4 * T - 1024, align_bytes=64)
-        nc.vector.tensor_copy(q_bf1[:], q_raw1[:].rearrange("p j w -> p w j"))
-        y = sb.tile([P, 2, N], F32, name="y")
+        q_bf1 = shared.tile([P, P, PACK], BF16, name="q_bf1", offset=14 * T, align_bytes=64)
+        nc.scalar.copy(q_bf1[:], q_raw1[:].rearrange("p j w -> p w j"))
+        y = shared.tile([P, 2, N], F32, name="y", offset=raw1 - 3072, align_bytes=64)
 
         def product(dst, stationary, moving):
             nc.tensor.matmul_mx(
@@ -173,8 +180,6 @@ def tile_attend_sigscat_topk_kernel(tc, qT, k_words, k_scales, kb, th, offs, out
             nc.vector.tensor_tensor(z[:], a[:], kb_rows[c][:], ALU.add)
             nc.scalar.activation(y[:, 0, chunk[c]], z[:], ACT.Sigmoid, bias=neg_th[:, 0:1])
         quantise(1, shared.tile([P, P], U32, name="q_code1", offset=late + 2048, align_bytes=64), q_bf1)
-        zeros = shared.tile([P, FILL], F32, name="zeros", offset=4 * T - 1024, align_bytes=64)
-        nc.gpsimd.memset(zeros[:], 0.0)
         nc.vector.tensor_copy(listed(map0[:], halves[0]), y[:, 0, halves[0]])
 
         def long_road(h, chunks, score_banks, turn_bank, turned):

@@ -65,11 +65,11 @@ def tile_attend_sigscat_topk_kernel(tc, qT, k_words, k_scales, kb, th, offs, out
         kb_pool = shared.tile([P, T], F32, name="kb_pool", offset=0, align_bytes=64)
         for cols in odd_pieces(KB_SPLIT):
             nc.vector.memset(kb_pool[0:KB_ROW, cols].bitcast(I32), 0)
-        nc.sync.dma_start(kb_pool[KB_ROW:P, :], kb[0:1, :])
 
         q_rows = qT[0].rearrange("(p j) w -> p j w", j=PACK)
         q_raw0 = sb.tile([P, PACK, P], F32, name="q_raw0")
         nc.sync.dma_start(q_raw0[:], q_rows[:, :, 0:P])
+        nc.sync.dma_start(kb_pool[KB_ROW:P, :], kb[0:1, :])
         th_rows = sb.tile([P, P], F32, name="th_rows")
         nc.sync.dma_start(th_rows[P - 2 : P, :], th[0].rearrange("(h p) o -> h (p o)", h=2))
         word_pool = sb.tile([P, T], I32, name="word_pool")

@@ -20,12 +20,9 @@ N = 512
 NQ = 256
 D = 512
 HALF = N // 2
-MAP1_EARLY = 384
-FILL = 96
 CHUNKS = N // P
 SCALE_ROW = P - 16
 KB_ROW = P - 1
-KB_SPLIT = 1664
 
 FLOPS = 2 * NQ * N * D
 BYTES = 4 * D * NQ + D * T + 16 * T + 4 * T + 4 * NQ + 2 * P * (N // 16) + 4 * NQ * T
@@ -59,102 +56,72 @@ def tile_attend_sigscat_topk_kernel(tc, qT, k_words, k_scales, kb, th, offs, out
         warm = sb.tile([P, 1], F32, name="warm")
         nc.scalar.activation(warm[:], warm_in[:], ACT.Sigmoid)
 
-        scale_pool = sb.tile([P, T // 4], I32, name="scale_pool", tag="scale_pool")
+        scale_pool = sb.tile([P, T // 4], I32, name="scale_pool")
         nc.gpsimd.memset(scale_pool[0:SCALE_ROW, :], 0)
         nc.sync.dma_start(scale_pool[SCALE_ROW:P, :], k_scales[0].bitcast(I32))
-        kb_pool = shared.tile([P, T], F32, name="kb_pool", offset=0, align_bytes=64)
-        for cols in odd_pieces(KB_SPLIT):
+        kb_pool = sb.tile([P, T], F32, name="kb_pool")
+        for cols in odd_pieces(T):
             nc.vector.memset(kb_pool[0:KB_ROW, cols].bitcast(I32), 0)
-
-        q_rows = qT[0].rearrange("(p j) w -> p j w", j=PACK)
-        q_raw0 = sb.tile([P, PACK, P], F32, name="q_raw0")
-        nc.sync.dma_start(q_raw0[:], q_rows[:, :, 0:P])
         nc.sync.dma_start(kb_pool[KB_ROW:P, :], kb[0:1, :])
+        q_raw = sb.tile([P, PACK, NQ], F32, name="q_raw")
+        nc.sync.dma_start(q_raw[:], qT[0].rearrange("(p j) w -> p j w", j=PACK))
         th_rows = sb.tile([P, P], F32, name="th_rows")
         nc.sync.dma_start(th_rows[P - 2 : P, :], th[0].rearrange("(h p) o -> h (p o)", h=2))
         word_pool = sb.tile([P, T], I32, name="word_pool")
-        words = k_words[0].rearrange("p t r -> p (t r)").bitcast(I32)
-        nc.sync.dma_start(word_pool[:], words)
-        raw1 = 12 * T
-        q_raw1 = shared.tile([P, PACK, P], F32, name="q_raw1", offset=raw1, align_bytes=64)
-        nc.sync.dma_start(q_raw1[:], q_rows[:, :, P:NQ])
+        nc.sync.dma_start(word_pool[:], k_words[0].rearrange("p t r -> p (t r)").bitcast(I32))
 
         ident = sb.tile([P, P], F32, name="ident")
         make_identity(nc, ident[:])
         nc.gpsimd.memset(th_rows[0 : P - 2, :], 0.0)
         k_scale = sb.tile([P, N], U8, name="k_scale", align_bytes=64)
         nc.gpsimd.memset(k_scale[:].bitcast(I32), 0)
-        nc.gpsimd.memset(kb_pool[0:KB_ROW, KB_SPLIT:T].bitcast(I32), 0)
         map0 = sb.tile([P, T], F32, name="map0")
         nc.gpsimd.memset(map0[:], 0.0)
-        map1 = sb.tile([P, T], F32, name="map1")
-        nc.gpsimd.memset(map1[:, 0:MAP1_EARLY], 0.0)
-
-        th_turned = bank(4, "th_turned", P)
-        nc.tensor.transpose(th_turned[:], th_rows[:], ident[:])
-        neg_th = sb.tile([P, 2], F32, name="neg_th")
-        nc.scalar.activation(neg_th[:], th_turned[:, P - 2 : P], ACT.Copy, scale=-1.0)
 
         scale_listed = sb.tile([P, N], U8, name="scale_listed")
         nc.vector.tensor_copy(scale_listed[:], scale_pool[:].bitcast(U8).indirect(offsets[:]))
         for quad in range(4):
             first = SCALE_ROW + 4 * quad
-            nc.scalar.dma_start(
+            nc.sync.dma_start(
                 k_scale[32 * quad : 32 * quad + 4, :].bitcast(I32), scale_listed[first : first + 4, :].bitcast(I32)
             )
 
-        kb_listed = shared.tile([P, N], F32, name="kb_listed", offset=4 * T, align_bytes=64)
-        for u in range(2):
-            nc.vector.tensor_copy(kb_listed[:, halves[u]], listed(kb_pool[:], halves[u]))
-
-        kb_col = sb.tile([P, CHUNKS], F32, name="kb_col")
-        late = 4 * T + 4 * N
-
-        kb_first = shared.tile([P, 1], F32, name="kb_first", offset=14 * T, align_bytes=64)
+        kb_listed = [sb.tile([P, HALF], F32, name="kb_listed%d" % u) for u in range(2)]
+        kb_col = [sb.tile([P, 2], F32, name="kb_col%d" % u) for u in range(2)]
 
         def turn_kb(u):
-            turned = bank(0, "kb_turned%d" % u, HALF)
+            nc.scalar.activation(kb_listed[u][:], listed(kb_pool[:], halves[u]), ACT.Copy)
+            turned = bank(u, "kb_turned%d" % u, HALF)
             for c in range(2):
-                nc.tensor.transpose(turned[:, chunk[c]], kb_listed[:, chunk[2 * u + c]], ident[:])
-            if u == 0:
-                nc.scalar.copy(kb_first[:], turned[:, KB_ROW:P])
-            nc.scalar.copy(kb_col[:, 2 * u : 2 * u + 2], turned[:].rearrange("p (c n) -> p c n", n=P)[:, :, KB_ROW])
+                nc.tensor.transpose(turned[:, chunk[c]], kb_listed[u][:, chunk[c]], ident[:])
+            nc.scalar.copy(kb_col[u][:], turned[:].rearrange("p (c n) -> p c n", n=P)[:, :, KB_ROW])
 
         turn_kb(0)
-        kb_rows = []
-        for c in range(2):
-            kb_spread = bank(2 + c, "kb_spread%d" % c, P)
-            nc.tensor.transpose(kb_spread[:], (kb_first[:], kb_col[:, 1:2])[c].to_broadcast([P, P]), ident[:])
-            rows = shared.tile([P, P], F32, name="kb_rows%d" % c, offset=late + (1920, 0)[c], align_bytes=64)
-            nc.scalar.copy(rows[:], kb_spread[:])
-            kb_rows.append(rows)
         turn_kb(1)
+        kb_spread = bank(2, "kb_spread", HALF)
+        for c in range(2):
+            nc.tensor.transpose(kb_spread[:, chunk[c]], kb_col[0][:, c : c + 1].to_broadcast([P, P]), ident[:])
+        kb_rows = shared.tile([P, HALF], F32, name="kb_rows", offset=4 * T, align_bytes=64)
+        nc.scalar.copy(kb_rows[:], kb_spread[:])
 
+        th_turned = bank(3, "th_turned", P)
+        nc.tensor.transpose(th_turned[:], th_rows[:], ident[:])
+        neg_th = sb.tile([P, 2], F32, name="neg_th")
+        nc.scalar.activation(neg_th[:], th_turned[:, P - 2 : P], ACT.Copy, scale=-1.0)
+
+        q_bf = shared.tile([P, NQ, PACK], BF16, name="q_bf", offset=0, align_bytes=64)
+        nc.vector.tensor_copy(q_bf[:], q_raw[:].rearrange("p j w -> p w j"))
+        q_code = sb.tile([P, NQ], U32, name="q_code", align_bytes=64)
         q_scale = sb.tile([P, NQ], U8, name="q_scale", align_bytes=64)
-        q_code = {}
+        nc.vector.quantize_mx(
+            out=q_code[:].bitcast(FP8X4), scales=q_scale[:], in_=q_bf[:].rearrange("p w j -> p (w j)")
+        )
+        map1 = shared.tile([P, T], F32, name="map1", offset=0, align_bytes=64)
+        nc.gpsimd.memset(map1[:], 0.0)
 
-        def quantise(h, codes, q_bf):
-            q_code[h] = codes
-            nc.vector.quantize_mx(
-                out=codes[:].bitcast(FP8X4),
-                scales=q_scale[:, chunk[h]],
-                in_=q_bf[:].rearrange("p w j -> p (w j)"),
-            )
-
-        q_bf0 = sb.tile([P, P, PACK], BF16, name="q_bf0", tag="wide", align_bytes=64)
-        nc.scalar.copy(q_bf0[:], q_raw0[:].rearrange("p j w -> p w j"))
-        quantise(0, shared.tile([P, P], U32, name="q_code0", offset=0, align_bytes=64), q_bf0)
-        zeros = sb.tile([P, FILL], F32, name="zeros", tag="wide", align_bytes=64)
-        nc.gpsimd.memset(zeros[:], 0.0)
-        nc.gpsimd.memset(map1[:, MAP1_EARLY:T], 0.0)
-
-        k_code = shared.tile([P, N], U32, name="k_code", offset=4 * P, align_bytes=64)
-        for u in range(2):
-            nc.vector.tensor_copy(k_code[:, halves[u]], listed(word_pool[:].bitcast(U32), halves[u]))
-
-        q_bf1 = shared.tile([P, P, PACK], BF16, name="q_bf1", offset=14 * T, align_bytes=64)
-        nc.scalar.copy(q_bf1[:], q_raw1[:].rearrange("p j w -> p w j"))
-        y = shared.tile([P, 2, N], F32, name="y", offset=raw1 - 3072, align_bytes=64)
+        k_code = sb.tile([P, N], U32, name="k_code", align_bytes=64)
+        for c in range(CHUNKS):
+            nc.vector.tensor_copy(k_code[:, chunk[c]], listed(word_pool[:].bitcast(U32), chunk[c]))
 
         def product(dst, stationary, moving):
             nc.tensor.matmul_mx(
@@ -167,40 +134,45 @@ def tile_attend_sigscat_topk_kernel(tc, qT, k_words, k_scales, kb, th, offs, out
                 stop=True,
             )
 
-        def queries(h):
-            return q_code[h][:], q_scale[:, chunk[h]]
+        def queries(cols):
+            return q_code[:, cols], q_scale[:, cols]
 
         def keys(cols):
             return k_code[:, cols], k_scale[:, cols]
 
+        y = [[sb.tile([P, HALF], F32, name="y%d_%d" % (h, u)) for u in range(2)] for h in range(2)]
+
+        def short_road(h, cols, b, place):
+            width = cols.stop - cols.start
+            a = bank(b, "a%d_%d" % (h, cols.start), width)
+            product(a[:], queries(chunk[h]), keys(cols))
+            z = shared.tile([P, width], F32, name="z%d_%d" % (h, cols.start), offset=place, align_bytes=64)
+            nc.vector.tensor_tensor(z[:], a[:], kb_rows[:, cols], ALU.add)
+            return z
+
         for c in range(2):
-            a = bank(4 + c, "a0_%d" % c, P)
-            product(a[:], queries(0), keys(chunk[c]))
-            z = shared.tile([P, P], F32, name="z0_%d" % c, offset=late + (2560, 512)[c], align_bytes=64)
-            nc.vector.tensor_tensor(z[:], a[:], kb_rows[c][:], ALU.add)
-            nc.scalar.activation(y[:, 0, chunk[c]], z[:], ACT.Sigmoid, bias=neg_th[:, 0:1])
-        quantise(1, shared.tile([P, P], U32, name="q_code1", offset=late + 2048, align_bytes=64), q_bf1)
-        nc.vector.tensor_copy(listed(map0[:], halves[0]), y[:, 0, halves[0]])
+            z = short_road(0, chunk[c], 4 + c, (6 + c) * T)
+            nc.scalar.activation(y[0][0][:, chunk[c]], z[:], ACT.Sigmoid, bias=neg_th[:, 0:1])
+        z1 = short_road(1, halves[0], 6, 8 * T)
+        nc.vector.tensor_copy(listed(map0[:], halves[0]), y[0][0][:])
 
-        def long_road(h, chunks, score_banks, turn_bank, turned):
-            for j, c in enumerate(chunks):
-                a = bank(score_banks[j], "a%d_%d" % (h, c), P)
-                product(a[:], keys(chunk[c]), queries(h))
-                nc.scalar.activation(turned[:, j, :], a[:], ACT.Identity, bias=kb_col[:, c : c + 1])
-            z = bank(turn_bank, "z%d_%d" % (h, chunks.start), len(chunks) * P)
-            for j, c in enumerate(chunks):
-                nc.tensor.transpose(z[:, chunk[j]], turned[:, j, :], ident[:])
-            cols = slice(chunks.start * P, chunks.stop * P)
-            nc.scalar.activation(y[:, h, cols], z[:], ACT.Sigmoid, bias=neg_th[:, h : h + 1])
-            return cols
+        turned = [shared.tile([P, NQ], F32, name="turned%d" % j, offset=(9, 7)[j] * T, align_bytes=64) for j in range(2)]
+        for j in range(2):
+            a = bank(j, "b%d" % j, NQ)
+            product(a[:], keys(chunk[2 + j]), queries(slice(0, NQ)))
+            nc.scalar.activation(turned[j][:], a[:], ACT.Identity, bias=kb_col[1][:, j : j + 1])
 
-        cols = long_road(1, range(0, 1), [2], 6, shared.tile([P, 1, P], F32, name="turned1a", offset=late + 256, align_bytes=64))
-        cols = slice(0, FILL)
-        nc.vector.tensor_tensor(listed(map1[:], cols), y[:, 1, cols], zeros[:], ALU.add)
-        cols = long_road(0, range(2, 4), [0, 1], 2, shared.tile([P, 2, P], F32, name="turned0", offset=late + 2816, align_bytes=64))
-        nc.vector.tensor_copy(listed(map0[:], cols), y[:, 0, cols])
+        def turn_back(h, b):
+            z = bank(b, "back%d" % h, HALF)
+            for j in range(2):
+                nc.tensor.transpose(z[:, chunk[j]], turned[j][:, chunk[h]], ident[:])
+            nc.scalar.activation(y[h][1][:], z[:], ACT.Sigmoid, bias=neg_th[:, h : h + 1])
+
+        turn_back(0, 2)
+        nc.vector.tensor_copy(listed(map0[:], halves[1]), y[0][1][:])
         nc.sync.dma_start(out[0, 0:P, :], map0[:])
-        cols = long_road(1, range(1, 4), [3, 4, 5], 0, shared.tile([P, 3, P], F32, name="turned1b", offset=late + 3328, align_bytes=64))
-        cols = slice(FILL, N)
-        nc.vector.tensor_copy(listed(map1[:], cols), y[:, 1, cols])
+        nc.scalar.activation(y[1][0][:], z1[:], ACT.Sigmoid, bias=neg_th[:, 1:2])
+        turn_back(1, 3)
+        nc.scalar.activation(listed(map1[:], halves[1]), y[1][1][:], ACT.Copy)
+        nc.vector.tensor_copy(listed(map1[:], halves[0]), y[1][0][:])
         nc.sync.dma_start(out[0, P:NQ, :], map1[:])

@@ -63,12 +63,15 @@ def tile_attend_sigscat_topk_kernel(tc, qT, k_words, k_scales, kb, th, offs, out
         for cols in odd_pieces(T):
             nc.vector.memset(kb_pool[0:KB_ROW, cols].bitcast(I32), 0)
         nc.sync.dma_start(kb_pool[KB_ROW:P, :], kb[0:1, :])
-        q_raw = sb.tile([P, PACK, NQ], F32, name="q_raw")
-        nc.sync.dma_start(q_raw[:], qT[0].rearrange("(p j) w -> p j w", j=PACK))
+        q_rows = qT[0].rearrange("(p j) w -> p j w", j=PACK)
+        q_raw0 = sb.tile([P, PACK, P], F32, name="q_raw0")
+        nc.sync.dma_start(q_raw0[:], q_rows[:, :, 0:P])
         th_rows = sb.tile([P, P], F32, name="th_rows")
         nc.sync.dma_start(th_rows[P - 2 : P, :], th[0].rearrange("(h p) o -> h (p o)", h=2))
         word_pool = sb.tile([P, T], I32, name="word_pool")
         nc.sync.dma_start(word_pool[:], k_words[0].rearrange("p t r -> p (t r)").bitcast(I32))
+        q_raw1 = shared.tile([P, PACK, P], F32, name="q_raw1", offset=11 * T, align_bytes=64)
+        nc.sync.dma_start(q_raw1[:], q_rows[:, :, P:NQ])
 
         ident = sb.tile([P, P], F32, name="ident")
         make_identity(nc, ident[:])
@@ -82,7 +85,7 @@ def tile_attend_sigscat_topk_kernel(tc, qT, k_words, k_scales, kb, th, offs, out
         nc.vector.tensor_copy(scale_listed[:], scale_pool[:].bitcast(U8).indirect(offsets[:]))
         for quad in range(4):
             first = SCALE_ROW + 4 * quad
-            nc.sync.dma_start(
+            nc.scalar.dma_start(
                 k_scale[32 * quad : 32 * quad + 4, :].bitcast(I32), scale_listed[first : first + 4, :].bitcast(I32)
             )
 
@@ -90,34 +93,39 @@ def tile_attend_sigscat_topk_kernel(tc, qT, k_words, k_scales, kb, th, offs, out
         kb_col = [sb.tile([P, 2], F32, name="kb_col%d" % u) for u in range(2)]
 
         def turn_kb(u):
-            nc.scalar.activation(kb_listed[u][:], listed(kb_pool[:], halves[u]), ACT.Copy)
+            if u == 0:
+                nc.scalar.activation(kb_listed[u][:], listed(kb_pool[:], halves[u]), ACT.Copy)
+            else:
+                nc.vector.tensor_copy(kb_listed[u][:], listed(kb_pool[:], halves[u]))
             turned = bank(u, "kb_turned%d" % u, HALF)
             for c in range(2):
                 nc.tensor.transpose(turned[:, chunk[c]], kb_listed[u][:, chunk[c]], ident[:])
             nc.scalar.copy(kb_col[u][:], turned[:].rearrange("p (c n) -> p c n", n=P)[:, :, KB_ROW])
 
         turn_kb(0)
-        turn_kb(1)
         kb_spread = bank(2, "kb_spread", HALF)
         for c in range(2):
             nc.tensor.transpose(kb_spread[:, chunk[c]], kb_col[0][:, c : c + 1].to_broadcast([P, P]), ident[:])
         kb_rows = shared.tile([P, HALF], F32, name="kb_rows", offset=4 * T, align_bytes=64)
         nc.scalar.copy(kb_rows[:], kb_spread[:])
+        turn_kb(1)
 
         th_turned = bank(3, "th_turned", P)
         nc.tensor.transpose(th_turned[:], th_rows[:], ident[:])
         neg_th = sb.tile([P, 2], F32, name="neg_th")
         nc.scalar.activation(neg_th[:], th_turned[:, P - 2 : P], ACT.Copy, scale=-1.0)
 
-        q_bf = shared.tile([P, NQ, PACK], BF16, name="q_bf", offset=0, align_bytes=64)
-        nc.vector.tensor_copy(q_bf[:], q_raw[:].rearrange("p j w -> p w j"))
-        q_code = sb.tile([P, NQ], U32, name="q_code", align_bytes=64)
         q_scale = sb.tile([P, NQ], U8, name="q_scale", align_bytes=64)
-        nc.vector.quantize_mx(
-            out=q_code[:].bitcast(FP8X4), scales=q_scale[:], in_=q_bf[:].rearrange("p w j -> p (w j)")
-        )
-        map1 = shared.tile([P, T], F32, name="map1", offset=0, align_bytes=64)
-        nc.gpsimd.memset(map1[:], 0.0)
+        q_code = sb.tile([P, NQ], U32, name="q_code", align_bytes=64)
+
+        def quantise(h, q_bf):
+            nc.vector.quantize_mx(
+                out=q_code[:, chunk[h]].bitcast(FP8X4), scales=q_scale[:, chunk[h]], in_=q_bf[:].rearrange("p w j -> p (w j)")
+            )
+
+        q_bf0 = sb.tile([P, P, PACK], BF16, name="q_bf0", align_bytes=64)
+        nc.vector.tensor_copy(q_bf0[:], q_raw0[:].rearrange("p j w -> p w j"))
+        quantise(0, q_bf0)
 
         k_code = sb.tile([P, N], U32, name="k_code", align_bytes=64)
         for c in range(CHUNKS):
@@ -140,7 +148,12 @@ def tile_attend_sigscat_topk_kernel(tc, qT, k_words, k_scales, kb, th, offs, out
         def keys(cols):
             return k_code[:, cols], k_scale[:, cols]
 
-        y = [[sb.tile([P, HALF], F32, name="y%d_%d" % (h, u)) for u in range(2)] for h in range(2)]
+        q_bf1 = shared.tile([P, P, PACK], BF16, name="q_bf1", offset=0, align_bytes=64)
+        nc.scalar.copy(q_bf1[:], q_raw1[:].rearrange("p j w -> p w j"))
+
+        quantise(1, q_bf1)
+        map1 = shared.tile([P, T], F32, name="map1", offset=0, align_bytes=64)
+        nc.gpsimd.memset(map1[:], 0.0)
 
         def short_road(h, cols, b, place):
             width = cols.stop - cols.start
@@ -150,11 +163,12 @@ def tile_attend_sigscat_topk_kernel(tc, qT, k_words, k_scales, kb, th, offs, out
             nc.vector.tensor_tensor(z[:], a[:], kb_rows[:, cols], ALU.add)
             return z
 
+        y00 = shared.tile([P, HALF], F32, name="y00", offset=11 * T, align_bytes=64)
         for c in range(2):
             z = short_road(0, chunk[c], 4 + c, (6 + c) * T)
-            nc.scalar.activation(y[0][0][:, chunk[c]], z[:], ACT.Sigmoid, bias=neg_th[:, 0:1])
+            nc.scalar.activation(y00[:, chunk[c]], z[:], ACT.Sigmoid, bias=neg_th[:, 0:1])
         z1 = short_road(1, halves[0], 6, 8 * T)
-        nc.vector.tensor_copy(listed(map0[:], halves[0]), y[0][0][:])
+        nc.vector.tensor_copy(listed(map0[:], halves[0]), y00[:])
 
         turned = [shared.tile([P, NQ], F32, name="turned%d" % j, offset=(9, 7)[j] * T, align_bytes=64) for j in range(2)]
         for j in range(2):
@@ -166,13 +180,16 @@ def tile_attend_sigscat_topk_kernel(tc, qT, k_words, k_scales, kb, th, offs, out
             z = bank(b, "back%d" % h, HALF)
             for j in range(2):
                 nc.tensor.transpose(z[:, chunk[j]], turned[j][:, chunk[h]], ident[:])
-            nc.scalar.activation(y[h][1][:], z[:], ACT.Sigmoid, bias=neg_th[:, h : h + 1])
+            y = sb.tile([P, HALF], F32, name="y%d1" % h)
+            nc.scalar.activation(y[:], z[:], ACT.Sigmoid, bias=neg_th[:, h : h + 1])
+            return y
 
-        turn_back(0, 2)
-        nc.vector.tensor_copy(listed(map0[:], halves[1]), y[0][1][:])
+        y01 = turn_back(0, 2)
+        nc.vector.tensor_copy(listed(map0[:], halves[1]), y01[:])
         nc.sync.dma_start(out[0, 0:P, :], map0[:])
-        nc.scalar.activation(y[1][0][:], z1[:], ACT.Sigmoid, bias=neg_th[:, 1:2])
-        turn_back(1, 3)
-        nc.scalar.activation(listed(map1[:], halves[1]), y[1][1][:], ACT.Copy)
-        nc.vector.tensor_copy(listed(map1[:], halves[0]), y[1][0][:])
+        y11 = turn_back(1, 3)
+        y10 = shared.tile([P, HALF], F32, name="y10", offset=9 * T, align_bytes=64)
+        nc.scalar.activation(y10[:], z1[:], ACT.Sigmoid, bias=neg_th[:, 1:2])
+        nc.scalar.activation(listed(map1[:], halves[0]), y10[:], ACT.Copy)
+        nc.vector.tensor_copy(listed(map1[:], halves[1]), y11[:])
         nc.sync.dma_start(out[0, P:NQ, :], map1[:])

@@ -23,6 +23,8 @@ HALF = N // 2
 CHUNKS = N // P
 SCALE_ROW = P - 16
 KB_ROW = P - 1
+KB_SPLIT = 1792
+LATE = 64
 
 FLOPS = 2 * NQ * N * D
 BYTES = 4 * D * NQ + D * T + 16 * T + 4 * T + 4 * NQ + 2 * P * (N // 16) + 4 * NQ * T
@@ -56,22 +58,20 @@ def tile_attend_sigscat_topk_kernel(tc, qT, k_words, k_scales, kb, th, offs, out
         warm = sb.tile([P, 1], F32, name="warm")
         nc.scalar.activation(warm[:], warm_in[:], ACT.Sigmoid)
 
-        scale_pool = sb.tile([P, T // 4], I32, name="scale_pool")
+        scale_pool = shared.tile([P, T // 4], I32, name="scale_pool", offset=12 * T, align_bytes=64)
         nc.gpsimd.memset(scale_pool[0:SCALE_ROW, :], 0)
         nc.sync.dma_start(scale_pool[SCALE_ROW:P, :], k_scales[0].bitcast(I32))
         kb_pool = sb.tile([P, T], F32, name="kb_pool")
-        for cols in odd_pieces(T):
+        nc.gpsimd.memset(kb_pool[0:KB_ROW, KB_SPLIT:T].bitcast(I32), 0)
+        for cols in odd_pieces(KB_SPLIT):
             nc.vector.memset(kb_pool[0:KB_ROW, cols].bitcast(I32), 0)
         nc.sync.dma_start(kb_pool[KB_ROW:P, :], kb[0:1, :])
-        q_rows = qT[0].rearrange("(p j) w -> p j w", j=PACK)
-        q_raw0 = sb.tile([P, PACK, P], F32, name="q_raw0")
-        nc.sync.dma_start(q_raw0[:], q_rows[:, :, 0:P])
+        q_raw = sb.tile([P, PACK, NQ], F32, name="q_raw")
+        nc.sync.dma_start(q_raw[:], qT[0].rearrange("(p j) w -> p j w", j=PACK))
         th_rows = sb.tile([P, P], F32, name="th_rows")
         nc.sync.dma_start(th_rows[P - 2 : P, :], th[0].rearrange("(h p) o -> h (p o)", h=2))
         word_pool = sb.tile([P, T], I32, name="word_pool")
         nc.sync.dma_start(word_pool[:], k_words[0].rearrange("p t r -> p (t r)").bitcast(I32))
-        q_raw1 = shared.tile([P, PACK, P], F32, name="q_raw1", offset=11 * T, align_bytes=64)
-        nc.sync.dma_start(q_raw1[:], q_rows[:, :, P:NQ])
 
         ident = sb.tile([P, P], F32, name="ident")
         make_identity(nc, ident[:])
@@ -89,11 +89,11 @@ def tile_attend_sigscat_topk_kernel(tc, qT, k_words, k_scales, kb, th, offs, out
                 k_scale[32 * quad : 32 * quad + 4, :].bitcast(I32), scale_listed[first : first + 4, :].bitcast(I32)
             )
 
-        kb_listed = [sb.tile([P, HALF], F32, name="kb_listed%d" % u) for u in range(2)]
+        kb_listed = [shared.tile([P, HALF], F32, name="kb_listed%d" % u, offset=(13, 12)[u] * T, align_bytes=64) for u in range(2)]
         kb_col = [sb.tile([P, 2], F32, name="kb_col%d" % u) for u in range(2)]
 
         def turn_kb(u):
-            if u == 0:
+            if u == 1:
                 nc.scalar.activation(kb_listed[u][:], listed(kb_pool[:], halves[u]), ACT.Copy)
             else:
                 nc.vector.tensor_copy(kb_listed[u][:], listed(kb_pool[:], halves[u]))
@@ -106,8 +106,8 @@ def tile_attend_sigscat_topk_kernel(tc, qT, k_words, k_scales, kb, th, offs, out
         kb_spread = bank(2, "kb_spread", HALF)
         for c in range(2):
             nc.tensor.transpose(kb_spread[:, chunk[c]], kb_col[0][:, c : c + 1].to_broadcast([P, P]), ident[:])
-        kb_rows = shared.tile([P, HALF], F32, name="kb_rows", offset=4 * T, align_bytes=64)
-        nc.scalar.copy(kb_rows[:], kb_spread[:])
+        kb_rows = shared.tile([P, N], F32, name="kb_rows", offset=4 * T, align_bytes=64)
+        nc.scalar.copy(kb_rows[:, halves[0]], kb_spread[:])
         turn_kb(1)
 
         th_turned = bank(3, "th_turned", P)
@@ -115,17 +115,21 @@ def tile_attend_sigscat_topk_kernel(tc, qT, k_words, k_scales, kb, th, offs, out
         neg_th = sb.tile([P, 2], F32, name="neg_th")
         nc.scalar.activation(neg_th[:], th_turned[:, P - 2 : P], ACT.Copy, scale=-1.0)
 
+        kb_spread = bank(7, "kb_spread1", HALF)
+        for c in range(2):
+            nc.tensor.transpose(kb_spread[:, chunk[c]], kb_col[1][:, c : c + 1].to_broadcast([P, P]), ident[:])
+        nc.scalar.copy(kb_rows[:, halves[1]], kb_spread[:])
+
         q_scale = sb.tile([P, NQ], U8, name="q_scale", align_bytes=64)
         q_code = sb.tile([P, NQ], U32, name="q_code", align_bytes=64)
 
-        def quantise(h, q_bf):
-            nc.vector.quantize_mx(
-                out=q_code[:, chunk[h]].bitcast(FP8X4), scales=q_scale[:, chunk[h]], in_=q_bf[:].rearrange("p w j -> p (w j)")
-            )
-
-        q_bf0 = sb.tile([P, P, PACK], BF16, name="q_bf0", align_bytes=64)
-        nc.vector.tensor_copy(q_bf0[:], q_raw0[:].rearrange("p j w -> p w j"))
-        quantise(0, q_bf0)
+        q_bf = shared.tile([P, NQ, PACK], BF16, name="q_bf", offset=0, align_bytes=64)
+        nc.vector.tensor_copy(q_bf[:], q_raw[:].rearrange("p j w -> p w j"))
+        nc.vector.quantize_mx(
+            out=q_code[:].bitcast(FP8X4), scales=q_scale[:], in_=q_bf[:].rearrange("p w j -> p (w j)")
+        )
+        map1 = shared.tile([P, T], F32, name="map1", offset=0, align_bytes=64)
+        nc.gpsimd.memset(map1[:], 0.0)
 
         k_code = sb.tile([P, N], U32, name="k_code", align_bytes=64)
         for c in range(CHUNKS):
@@ -148,13 +152,6 @@ def tile_attend_sigscat_topk_kernel(tc, qT, k_words, k_scales, kb, th, offs, out
         def keys(cols):
             return k_code[:, cols], k_scale[:, cols]
 
-        q_bf1 = shared.tile([P, P, PACK], BF16, name="q_bf1", offset=0, align_bytes=64)
-        nc.scalar.copy(q_bf1[:], q_raw1[:].rearrange("p j w -> p w j"))
-
-        quantise(1, q_bf1)
-        map1 = shared.tile([P, T], F32, name="map1", offset=0, align_bytes=64)
-        nc.gpsimd.memset(map1[:], 0.0)
-
         def short_road(h, cols, b, place):
             width = cols.stop - cols.start
             a = bank(b, "a%d_%d" % (h, cols.start), width)
@@ -170,26 +167,25 @@ def tile_attend_sigscat_topk_kernel(tc, qT, k_words, k_scales, kb, th, offs, out
         z1 = short_road(1, halves[0], 6, 8 * T)
         nc.vector.tensor_copy(listed(map0[:], halves[0]), y00[:])
 
-        turned = [shared.tile([P, NQ], F32, name="turned%d" % j, offset=(9, 7)[j] * T, align_bytes=64) for j in range(2)]
+        y10 = shared.tile([P, HALF + LATE], F32, name="y10", offset=7 * T + 256, align_bytes=64)
+        turned0 = sb.tile([P, P], F32, name="turned0")
+        turned = [turned0[:], y10[:, HALF - LATE : HALF + LATE]]
         for j in range(2):
-            a = bank(j, "b%d" % j, NQ)
-            product(a[:], keys(chunk[2 + j]), queries(slice(0, NQ)))
-            nc.scalar.activation(turned[j][:], a[:], ACT.Identity, bias=kb_col[1][:, j : j + 1])
-
-        def turn_back(h, b):
-            z = bank(b, "back%d" % h, HALF)
-            for j in range(2):
-                nc.tensor.transpose(z[:, chunk[j]], turned[j][:, chunk[h]], ident[:])
-            y = sb.tile([P, HALF], F32, name="y%d1" % h)
-            nc.scalar.activation(y[:], z[:], ACT.Sigmoid, bias=neg_th[:, h : h + 1])
-            return y
-
-        y01 = turn_back(0, 2)
+            a = bank(j, "b%d" % j, P)
+            product(a[:], keys(chunk[2 + j]), queries(chunk[0]))
+            nc.scalar.activation(turned[j], a[:], ACT.Identity, bias=kb_col[1][:, j : j + 1])
+        back = bank(2, "back", HALF)
+        for j in range(2):
+            nc.tensor.transpose(back[:, chunk[j]], turned[j], ident[:])
+        for cols in (slice(0, HALF - LATE), slice(HALF - LATE, HALF)):
+            nc.scalar.activation(y10[:, cols], z1[:, cols], ACT.Sigmoid, bias=neg_th[:, 1:2])
+        y01 = sb.tile([P, HALF], F32, name="y01")
+        nc.scalar.activation(y01[:], back[:], ACT.Sigmoid, bias=neg_th[:, 0:1])
+        z2 = short_road(1, halves[1], 3, 7 * T - 768)
         nc.vector.tensor_copy(listed(map0[:], halves[1]), y01[:])
         nc.sync.dma_start(out[0, 0:P, :], map0[:])
-        y11 = turn_back(1, 3)
-        y10 = shared.tile([P, HALF], F32, name="y10", offset=9 * T, align_bytes=64)
-        nc.scalar.activation(y10[:], z1[:], ACT.Sigmoid, bias=neg_th[:, 1:2])
-        nc.scalar.activation(listed(map1[:], halves[0]), y10[:], ACT.Copy)
+        nc.scalar.activation(listed(map1[:], halves[0]), y10[:, halves[0]], ACT.Copy)
+        y11 = shared.tile([P, HALF], F32, name="y11", offset=7 * T + 256, align_bytes=64)
+        nc.scalar.activation(y11[:], z2[:], ACT.Sigmoid, bias=neg_th[:, 1:2])
         nc.vector.tensor_copy(listed(map1[:], halves[1]), y11[:])
         nc.sync.dma_start(out[0, P:NQ, :], map1[:])

@@ -24,7 +24,7 @@ CHUNKS = N // P
 SCALE_ROW = P - 16
 KB_ROW = P - 1
 KB_SPLIT = 1792
-LATE = 64
+MAP1_EARLY = 1664
 
 FLOPS = 2 * NQ * N * D
 BYTES = 4 * D * NQ + D * T + 16 * T + 4 * T + 4 * NQ + 2 * P * (N // 16) + 4 * NQ * T
@@ -78,8 +78,8 @@ def tile_attend_sigscat_topk_kernel(tc, qT, k_words, k_scales, kb, th, offs, out
         nc.gpsimd.memset(th_rows[0 : P - 2, :], 0.0)
         k_scale = sb.tile([P, N], U8, name="k_scale", align_bytes=64)
         nc.gpsimd.memset(k_scale[:].bitcast(I32), 0)
-        map0 = sb.tile([P, T], F32, name="map0")
-        nc.gpsimd.memset(map0[:], 0.0)
+        map1 = sb.tile([P, T], F32, name="map1")
+        nc.gpsimd.memset(map1[:, 0:MAP1_EARLY], 0.0)
 
         scale_listed = sb.tile([P, N], U8, name="scale_listed")
         nc.vector.tensor_copy(scale_listed[:], scale_pool[:].bitcast(U8).indirect(offsets[:]))
@@ -89,47 +89,50 @@ def tile_attend_sigscat_topk_kernel(tc, qT, k_words, k_scales, kb, th, offs, out
                 k_scale[32 * quad : 32 * quad + 4, :].bitcast(I32), scale_listed[first : first + 4, :].bitcast(I32)
             )
 
-        kb_listed = [shared.tile([P, HALF], F32, name="kb_listed%d" % u, offset=(13, 12)[u] * T, align_bytes=64) for u in range(2)]
-        kb_col = [sb.tile([P, 2], F32, name="kb_col%d" % u) for u in range(2)]
-
-        def turn_kb(u):
-            if u == 1:
-                nc.scalar.activation(kb_listed[u][:], listed(kb_pool[:], halves[u]), ACT.Copy)
-            else:
-                nc.vector.tensor_copy(kb_listed[u][:], listed(kb_pool[:], halves[u]))
-            turned = bank(u, "kb_turned%d" % u, HALF)
-            for c in range(2):
-                nc.tensor.transpose(turned[:, chunk[c]], kb_listed[u][:, chunk[c]], ident[:])
-            nc.scalar.copy(kb_col[u][:], turned[:].rearrange("p (c n) -> p c n", n=P)[:, :, KB_ROW])
-
-        turn_kb(0)
-        kb_spread = bank(2, "kb_spread", HALF)
+        kb_rows = shared.tile([P, HALF], F32, name="kb_rows", offset=4 * T, align_bytes=64)
+        first_cols = []
         for c in range(2):
-            nc.tensor.transpose(kb_spread[:, chunk[c]], kb_col[0][:, c : c + 1].to_broadcast([P, P]), ident[:])
-        kb_rows = shared.tile([P, N], F32, name="kb_rows", offset=4 * T, align_bytes=64)
-        nc.scalar.copy(kb_rows[:, halves[0]], kb_spread[:])
-        turn_kb(1)
+            listed_kb = sb.tile([P, P], F32, name="kb_listed%d" % c)
+            nc.vector.tensor_copy(listed_kb[:], listed(kb_pool[:], chunk[c]))
+            turned = bank(4 + c, "kb_turned%d" % c, P)
+            nc.tensor.transpose(turned[:], listed_kb[:], ident[:])
+            col = sb.tile([P, 1], F32, name="kb_col%d" % c)
+            nc.scalar.copy(col[:], turned[:, KB_ROW:P])
+            first_cols.append(col)
+        for c in range(2):
+            spread = bank(c, "kb_spread%d" % c, P)
+            nc.tensor.transpose(spread[:], first_cols[c][:].to_broadcast([P, P]), ident[:])
+            nc.scalar.copy(kb_rows[:, chunk[c]], spread[:])
+
+        listed_kb = shared.tile([P, HALF], F32, name="kb_listed_late", offset=12 * T, align_bytes=64)
+        nc.scalar.activation(listed_kb[:], listed(kb_pool[:], halves[1]), ACT.Copy)
+        turned = bank(2, "kb_turned_late", HALF)
+        for c in range(2):
+            nc.tensor.transpose(turned[:, chunk[c]], listed_kb[:, chunk[c]], ident[:])
+        late_cols = sb.tile([P, 2], F32, name="late_cols")
+        nc.scalar.copy(late_cols[:], turned[:].rearrange("p (c n) -> p c n", n=P)[:, :, KB_ROW])
 
         th_turned = bank(3, "th_turned", P)
         nc.tensor.transpose(th_turned[:], th_rows[:], ident[:])
         neg_th = sb.tile([P, 2], F32, name="neg_th")
         nc.scalar.activation(neg_th[:], th_turned[:, P - 2 : P], ACT.Copy, scale=-1.0)
 
-        kb_spread = bank(7, "kb_spread1", HALF)
-        for c in range(2):
-            nc.tensor.transpose(kb_spread[:, chunk[c]], kb_col[1][:, c : c + 1].to_broadcast([P, P]), ident[:])
-        nc.scalar.copy(kb_rows[:, halves[1]], kb_spread[:])
-
         q_scale = sb.tile([P, NQ], U8, name="q_scale", align_bytes=64)
         q_code = sb.tile([P, NQ], U32, name="q_code", align_bytes=64)
 
         q_bf = shared.tile([P, NQ, PACK], BF16, name="q_bf", offset=0, align_bytes=64)
-        nc.vector.tensor_copy(q_bf[:], q_raw[:].rearrange("p j w -> p w j"))
-        nc.vector.quantize_mx(
-            out=q_code[:].bitcast(FP8X4), scales=q_scale[:], in_=q_bf[:].rearrange("p w j -> p (w j)")
-        )
-        map1 = shared.tile([P, T], F32, name="map1", offset=0, align_bytes=64)
-        nc.gpsimd.memset(map1[:], 0.0)
+        q_dealt = q_raw[:].rearrange("p j w -> p w j")
+        for h in range(2):
+            nc.vector.tensor_copy(q_bf[:, chunk[h], :], q_dealt[:, chunk[h], :])
+        for h in range(2):
+            nc.vector.quantize_mx(
+                out=q_code[:, chunk[h]].bitcast(FP8X4),
+                scales=q_scale[:, chunk[h]],
+                in_=q_bf[:, chunk[h], :].rearrange("p w j -> p (w j)"),
+            )
+        map0 = shared.tile([P, T], F32, name="map0", offset=0, align_bytes=64)
+        nc.gpsimd.memset(map0[:], 0.0)
+        nc.gpsimd.memset(map1[:, MAP1_EARLY:T], 0.0)
 
         k_code = sb.tile([P, N], U32, name="k_code", align_bytes=64)
         for c in range(CHUNKS):
@@ -167,25 +170,34 @@ def tile_attend_sigscat_topk_kernel(tc, qT, k_words, k_scales, kb, th, offs, out
         z1 = short_road(1, halves[0], 6, 8 * T)
         nc.vector.tensor_copy(listed(map0[:], halves[0]), y00[:])
 
-        y10 = shared.tile([P, HALF + LATE], F32, name="y10", offset=7 * T + 256, align_bytes=64)
-        turned0 = sb.tile([P, P], F32, name="turned0")
-        turned = [turned0[:], y10[:, HALF - LATE : HALF + LATE]]
+        turned0 = [shared.tile([P, P], F32, name="turned0_%d" % j, offset=(9 * T, 7 * T - 256)[j], align_bytes=64) for j in range(2)]
+        turned1 = shared.tile([P, 2, P], F32, name="turned1", offset=7 * T + 256, align_bytes=64)
+        turned = [[turned0[j][:] for j in range(2)], [turned1[:, j, :] for j in range(2)]]
         for j in range(2):
-            a = bank(j, "b%d" % j, P)
+            a = bank(j, "b0_%d" % j, P)
             product(a[:], keys(chunk[2 + j]), queries(chunk[0]))
-            nc.scalar.activation(turned[j], a[:], ACT.Identity, bias=kb_col[1][:, j : j + 1])
-        back = bank(2, "back", HALF)
+            nc.scalar.activation(turned[0][j], a[:], ACT.Identity, bias=late_cols[:, j : j + 1])
+        a = bank(7, "b1", HALF)
         for j in range(2):
-            nc.tensor.transpose(back[:, chunk[j]], turned[j], ident[:])
-        for cols in (slice(0, HALF - LATE), slice(HALF - LATE, HALF)):
-            nc.scalar.activation(y10[:, cols], z1[:, cols], ACT.Sigmoid, bias=neg_th[:, 1:2])
+            product(a[:, chunk[j]], keys(chunk[2 + j]), queries(chunk[1]))
+        for j in range(2):
+            nc.scalar.activation(turned[1][j], a[:, chunk[j]], ACT.Identity, bias=late_cols[:, j : j + 1])
+
+        def turn_back(h, b):
+            z = bank(b, "back%d" % h, HALF)
+            for j in range(2):
+                nc.tensor.transpose(z[:, chunk[j]], turned[h][j], ident[:])
+            return z
+
         y01 = sb.tile([P, HALF], F32, name="y01")
-        nc.scalar.activation(y01[:], back[:], ACT.Sigmoid, bias=neg_th[:, 0:1])
-        z2 = short_road(1, halves[1], 3, 7 * T - 768)
+        nc.scalar.activation(y01[:], turn_back(0, 2)[:], ACT.Sigmoid, bias=neg_th[:, 0:1])
         nc.vector.tensor_copy(listed(map0[:], halves[1]), y01[:])
         nc.sync.dma_start(out[0, 0:P, :], map0[:])
-        nc.scalar.activation(listed(map1[:], halves[0]), y10[:, halves[0]], ACT.Copy)
-        y11 = shared.tile([P, HALF], F32, name="y11", offset=7 * T + 256, align_bytes=64)
-        nc.scalar.activation(y11[:], z2[:], ACT.Sigmoid, bias=neg_th[:, 1:2])
+        back1 = turn_back(1, 3)
+        y10 = shared.tile([P, HALF], F32, name="y10", offset=7 * T + 512, align_bytes=64)
+        nc.scalar.activation(y10[:], z1[:], ACT.Sigmoid, bias=neg_th[:, 1:2])
+        y11 = sb.tile([P, HALF], F32, name="y11")
+        nc.scalar.activation(y11[:], back1[:], ACT.Sigmoid, bias=neg_th[:, 1:2])
+        nc.scalar.activation(listed(map1[:], halves[0]), y10[:], ACT.Copy)
         nc.vector.tensor_copy(listed(map1[:], halves[1]), y11[:])
         nc.sync.dma_start(out[0, P:NQ, :], map1[:])

@@ -21,10 +21,10 @@ NQ = 256
 D = 512
 HALF = N // 2
 CHUNKS = N // P
-SCALE_ROW = P - 16
+SCALE_ROW = P // 2 - 16
 KB_ROW = P - 1
 KB_SPLIT = 1792
-MAP1_EARLY = 1664
+MAP1_EARLY = 1152
 
 FLOPS = 2 * NQ * N * D
 BYTES = 4 * D * NQ + D * T + 16 * T + 4 * T + 4 * NQ + 2 * P * (N // 16) + 4 * NQ * T
@@ -60,7 +60,8 @@ def tile_attend_sigscat_topk_kernel(tc, qT, k_words, k_scales, kb, th, offs, out
 
         scale_pool = shared.tile([P, T // 4], I32, name="scale_pool", offset=12 * T, align_bytes=64)
         nc.gpsimd.memset(scale_pool[0:SCALE_ROW, :], 0)
-        nc.sync.dma_start(scale_pool[SCALE_ROW:P, :], k_scales[0].bitcast(I32))
+        nc.gpsimd.memset(scale_pool[P // 2 : P, :], 0)
+        nc.sync.dma_start(scale_pool[SCALE_ROW : P // 2, :], k_scales[0].bitcast(I32))
         kb_pool = sb.tile([P, T], F32, name="kb_pool")
         nc.gpsimd.memset(kb_pool[0:KB_ROW, KB_SPLIT:T].bitcast(I32), 0)
         for cols in odd_pieces(KB_SPLIT):
@@ -68,10 +69,10 @@ def tile_attend_sigscat_topk_kernel(tc, qT, k_words, k_scales, kb, th, offs, out
         nc.sync.dma_start(kb_pool[KB_ROW:P, :], kb[0:1, :])
         q_raw = sb.tile([P, PACK, NQ], F32, name="q_raw")
         nc.sync.dma_start(q_raw[:], qT[0].rearrange("(p j) w -> p j w", j=PACK))
-        th_rows = sb.tile([P, P], F32, name="th_rows")
-        nc.sync.dma_start(th_rows[P - 2 : P, :], th[0].rearrange("(h p) o -> h (p o)", h=2))
         word_pool = sb.tile([P, T], I32, name="word_pool")
         nc.sync.dma_start(word_pool[:], k_words[0].rearrange("p t r -> p (t r)").bitcast(I32))
+        th_rows = sb.tile([P, P], F32, name="th_rows")
+        nc.sync.dma_start(th_rows[P - 2 : P, :], th[0].rearrange("(h p) o -> h (p o)", h=2))
 
         ident = sb.tile([P, P], F32, name="ident")
         make_identity(nc, ident[:])

@@ -69,10 +69,10 @@ def tile_attend_sigscat_topk_kernel(tc, qT, k_words, k_scales, kb, th, offs, out
         nc.sync.dma_start(kb_pool[KB_ROW:P, :], kb[0:1, :])
         q_raw = sb.tile([P, PACK, NQ], F32, name="q_raw")
         nc.sync.dma_start(q_raw[:], qT[0].rearrange("(p j) w -> p j w", j=PACK))
-        word_pool = sb.tile([P, T], I32, name="word_pool")
-        nc.sync.dma_start(word_pool[:], k_words[0].rearrange("p t r -> p (t r)").bitcast(I32))
         th_rows = sb.tile([P, P], F32, name="th_rows")
         nc.sync.dma_start(th_rows[P - 2 : P, :], th[0].rearrange("(h p) o -> h (p o)", h=2))
+        word_pool = sb.tile([P, T], I32, name="word_pool")
+        nc.sync.dma_start(word_pool[:], k_words[0].rearrange("p t r -> p (t r)").bitcast(I32))
 
         ident = sb.tile([P, P], F32, name="ident")
         make_identity(nc, ident[:])
@@ -83,12 +83,20 @@ def tile_attend_sigscat_topk_kernel(tc, qT, k_words, k_scales, kb, th, offs, out
         nc.gpsimd.memset(map1[:, 0:MAP1_EARLY], 0.0)
 
         scale_listed = sb.tile([P, N], U8, name="scale_listed")
-        nc.vector.tensor_copy(scale_listed[:], scale_pool[:].bitcast(U8).indirect(offsets[:]))
-        for quad in range(4):
+
+        def move_scales(quad, cols):
             first = SCALE_ROW + 4 * quad
             nc.scalar.dma_start(
-                k_scale[32 * quad : 32 * quad + 4, :].bitcast(I32), scale_listed[first : first + 4, :].bitcast(I32)
+                k_scale[32 * quad : 32 * quad + 4, cols].bitcast(I32), scale_listed[first : first + 4, cols].bitcast(I32)
             )
+
+        nc.vector.tensor_copy(scale_listed[:, halves[0]], listed(scale_pool[:].bitcast(U8), halves[0]))
+        for quad in range(3):
+            move_scales(quad, halves[0])
+        nc.vector.tensor_copy(scale_listed[:, halves[1]], listed(scale_pool[:].bitcast(U8), halves[1]))
+        move_scales(3, slice(0, N))
+        for quad in range(3):
+            move_scales(quad, halves[1])
 
         kb_rows = shared.tile([P, HALF], F32, name="kb_rows", offset=4 * T, align_bytes=64)
         first_cols = []

from contextlib import ExitStack

import concourse.mybir as mybir
from concourse.masks import make_identity

F32 = mybir.dt.float32
BF16 = mybir.dt.bfloat16
I32 = mybir.dt.int32
U32 = mybir.dt.uint32
U16 = mybir.dt.uint16
U8 = mybir.dt.uint8
FP8X4 = mybir.dt.float8_e4m3fn_x4
ACT = mybir.ActivationFunctionType
ALU = mybir.AluOpType

P = 128
PACK = 4
T = 2048
N = 512
NQ = 256
D = 512
HALF = N // 2
CHUNKS = N // P
SCALE_ROW = P // 2 - 16
KB_ROW = P - 1
KB_SPLIT = 1792
MAP1_EARLY = 1152

FLOPS = 2 * NQ * N * D
BYTES = 4 * D * NQ + D * T + 16 * T + 4 * T + 4 * NQ + 2 * P * (N // 16) + 4 * NQ * T


def odd_pieces(width):
    return [slice(0, width // 2 - 1), slice(width // 2 - 1, width)]


def tile_attend_sigscat_topk_kernel(tc, qT, k_words, k_scales, kb, th, offs, out):
    nc = tc.nc
    with ExitStack() as ctx:
        sb = ctx.enter_context(tc.tile_pool(name="sb", bufs=1))
        shared = ctx.enter_context(tc.tile_pool(name="shared", bufs=1))
        ps = ctx.enter_context(tc.psum_pool(name="ps", bufs=1))

        def bank(b, name, width):
            return ps.tile([P, width], F32, name=name, tag="bank%d" % b)

        offsets = sb.tile([P, N // 16], U16, name="offsets")
        nc.sync.dma_start(offsets[:], offs)

        def listed(window, cols):
            return window.indirect(offsets[:, cols.start // 16 : cols.stop // 16])

        halves = [slice(u * HALF, (u + 1) * HALF) for u in range(2)]
        chunk = [slice(c * P, (c + 1) * P) for c in range(CHUNKS)]

        warm_in = sb.tile([P, 1], F32, name="warm_in")
        nc.vector.memset(warm_in[:], 0.0)
        warm = sb.tile([P, 1], F32, name="warm")
        nc.scalar.activation(warm[:], warm_in[:], ACT.Sigmoid)

        scale_pool = shared.tile([P, T // 4], I32, name="scale_pool", offset=12 * T, align_bytes=64)
        nc.gpsimd.memset(scale_pool[0:SCALE_ROW, :], 0)
        nc.gpsimd.memset(scale_pool[P // 2 : P, :], 0)
        nc.sync.dma_start(scale_pool[SCALE_ROW : P // 2, :], k_scales[0].bitcast(I32))
        kb_pool = sb.tile([P, T], F32, name="kb_pool")
        nc.gpsimd.memset(kb_pool[0:KB_ROW, KB_SPLIT:T].bitcast(I32), 0)
        for cols in odd_pieces(KB_SPLIT):
            nc.vector.memset(kb_pool[0:KB_ROW, cols].bitcast(I32), 0)
        nc.sync.dma_start(kb_pool[KB_ROW:P, :], kb[0:1, :])
        q_raw = sb.tile([P, PACK, NQ], F32, name="q_raw")
        nc.sync.dma_start(q_raw[:], qT[0].rearrange("(p j) w -> p j w", j=PACK))
        th_rows = sb.tile([P, P], F32, name="th_rows")
        nc.sync.dma_start(th_rows[P - 2 : P, :], th[0].rearrange("(h p) o -> h (p o)", h=2))
        word_pool = sb.tile([P, T], I32, name="word_pool")
        nc.sync.dma_start(word_pool[:], k_words[0].rearrange("p t r -> p (t r)").bitcast(I32))

        ident = sb.tile([P, P], F32, name="ident")
        make_identity(nc, ident[:])
        nc.gpsimd.memset(th_rows[0 : P - 2, :], 0.0)
        k_scale = sb.tile([P, N], U8, name="k_scale", align_bytes=64)
        nc.gpsimd.memset(k_scale[:].bitcast(I32), 0)
        map1 = sb.tile([P, T], F32, name="map1")
        nc.gpsimd.memset(map1[:, 0:MAP1_EARLY], 0.0)

        scale_listed = sb.tile([P, N], U8, name="scale_listed")

        def move_scales(quad, cols):
            first = SCALE_ROW + 4 * quad
            nc.scalar.dma_start(
                k_scale[32 * quad : 32 * quad + 4, cols].bitcast(I32), scale_listed[first : first + 4, cols].bitcast(I32)
            )

        nc.vector.tensor_copy(scale_listed[:, halves[0]], listed(scale_pool[:].bitcast(U8), halves[0]))
        for quad in range(3):
            move_scales(quad, halves[0])
        nc.vector.tensor_copy(scale_listed[:, halves[1]], listed(scale_pool[:].bitcast(U8), halves[1]))
        move_scales(3, slice(0, N))
        for quad in range(3):
            move_scales(quad, halves[1])

        kb_rows = shared.tile([P, HALF], F32, name="kb_rows", offset=4 * T, align_bytes=64)
        first_cols = []
        for c in range(2):
            listed_kb = sb.tile([P, P], F32, name="kb_listed%d" % c)
            nc.vector.tensor_copy(listed_kb[:], listed(kb_pool[:], chunk[c]))
            turned = bank(4 + c, "kb_turned%d" % c, P)
            nc.tensor.transpose(turned[:], listed_kb[:], ident[:])
            col = sb.tile([P, 1], F32, name="kb_col%d" % c)
            nc.scalar.copy(col[:], turned[:, KB_ROW:P])
            first_cols.append(col)
        for c in range(2):
            spread = bank(c, "kb_spread%d" % c, P)
            nc.tensor.transpose(spread[:], first_cols[c][:].to_broadcast([P, P]), ident[:])
            nc.scalar.copy(kb_rows[:, chunk[c]], spread[:])

        listed_kb = shared.tile([P, HALF], F32, name="kb_listed_late", offset=12 * T, align_bytes=64)
        nc.scalar.activation(listed_kb[:], listed(kb_pool[:], halves[1]), ACT.Copy)
        turned = bank(2, "kb_turned_late", HALF)
        for c in range(2):
            nc.tensor.transpose(turned[:, chunk[c]], listed_kb[:, chunk[c]], ident[:])
        late_cols = sb.tile([P, 2], F32, name="late_cols")
        nc.scalar.copy(late_cols[:], turned[:].rearrange("p (c n) -> p c n", n=P)[:, :, KB_ROW])

        th_turned = bank(3, "th_turned", P)
        nc.tensor.transpose(th_turned[:], th_rows[:], ident[:])
        neg_th = sb.tile([P, 2], F32, name="neg_th")
        nc.scalar.activation(neg_th[:], th_turned[:, P - 2 : P], ACT.Copy, scale=-1.0)

        q_scale = sb.tile([P, NQ], U8, name="q_scale", align_bytes=64)
        q_code = sb.tile([P, NQ], U32, name="q_code", align_bytes=64)

        q_bf = shared.tile([P, NQ, PACK], BF16, name="q_bf", offset=0, align_bytes=64)
        q_dealt = q_raw[:].rearrange("p j w -> p w j")
        for h in range(2):
            nc.vector.tensor_copy(q_bf[:, chunk[h], :], q_dealt[:, chunk[h], :])
        for h in range(2):
            nc.vector.quantize_mx(
                out=q_code[:, chunk[h]].bitcast(FP8X4),
                scales=q_scale[:, chunk[h]],
                in_=q_bf[:, chunk[h], :].rearrange("p w j -> p (w j)"),
            )
        map0 = shared.tile([P, T], F32, name="map0", offset=0, align_bytes=64)
        nc.gpsimd.memset(map0[:], 0.0)
        nc.gpsimd.memset(map1[:, MAP1_EARLY:T], 0.0)

        k_code = sb.tile([P, N], U32, name="k_code", align_bytes=64)
        for c in range(CHUNKS):
            nc.vector.tensor_copy(k_code[:, chunk[c]], listed(word_pool[:].bitcast(U32), chunk[c]))

        def product(dst, stationary, moving):
            nc.tensor.matmul_mx(
                out=dst,
                lhsT=stationary[0].bitcast(FP8X4),
                lhsT_scale=stationary[1],
                rhs=moving[0].bitcast(FP8X4),
                rhs_scale=moving[1],
                start=True,
                stop=True,
            )

        def queries(cols):
            return q_code[:, cols], q_scale[:, cols]

        def keys(cols):
            return k_code[:, cols], k_scale[:, cols]

        def short_road(h, cols, b, place):
            width = cols.stop - cols.start
            a = bank(b, "a%d_%d" % (h, cols.start), width)
            product(a[:], queries(chunk[h]), keys(cols))
            z = shared.tile([P, width], F32, name="z%d_%d" % (h, cols.start), offset=place, align_bytes=64)
            nc.vector.tensor_tensor(z[:], a[:], kb_rows[:, cols], ALU.add)
            return z

        y00 = shared.tile([P, HALF], F32, name="y00", offset=11 * T, align_bytes=64)
        for c in range(2):
            z = short_road(0, chunk[c], 4 + c, (6 + c) * T)
            nc.scalar.activation(y00[:, chunk[c]], z[:], ACT.Sigmoid, bias=neg_th[:, 0:1])
        z1 = short_road(1, halves[0], 6, 8 * T)
        nc.vector.tensor_copy(listed(map0[:], halves[0]), y00[:])

        turned0 = [shared.tile([P, P], F32, name="turned0_%d" % j, offset=(9 * T, 7 * T - 256)[j], align_bytes=64) for j in range(2)]
        turned1 = shared.tile([P, 2, P], F32, name="turned1", offset=7 * T + 256, align_bytes=64)
        turned = [[turned0[j][:] for j in range(2)], [turned1[:, j, :] for j in range(2)]]
        for j in range(2):
            a = bank(j, "b0_%d" % j, P)
            product(a[:], keys(chunk[2 + j]), queries(chunk[0]))
            nc.scalar.activation(turned[0][j], a[:], ACT.Identity, bias=late_cols[:, j : j + 1])
        a = bank(7, "b1", HALF)
        for j in range(2):
            product(a[:, chunk[j]], keys(chunk[2 + j]), queries(chunk[1]))
        for j in range(2):
            nc.scalar.activation(turned[1][j], a[:, chunk[j]], ACT.Identity, bias=late_cols[:, j : j + 1])

        def turn_back(h, b):
            z = bank(b, "back%d" % h, HALF)
            for j in range(2):
                nc.tensor.transpose(z[:, chunk[j]], turned[h][j], ident[:])
            return z

        y01 = sb.tile([P, HALF], F32, name="y01")
        nc.scalar.activation(y01[:], turn_back(0, 2)[:], ACT.Sigmoid, bias=neg_th[:, 0:1])
        nc.vector.tensor_copy(listed(map0[:], halves[1]), y01[:])
        nc.sync.dma_start(out[0, 0:P, :], map0[:])
        back1 = turn_back(1, 3)
        y10 = shared.tile([P, HALF], F32, name="y10", offset=7 * T + 512, align_bytes=64)
        nc.scalar.activation(y10[:], z1[:], ACT.Sigmoid, bias=neg_th[:, 1:2])
        y11 = sb.tile([P, HALF], F32, name="y11")
        nc.scalar.activation(y11[:], back1[:], ACT.Sigmoid, bias=neg_th[:, 1:2])
        nc.scalar.activation(listed(map1[:], halves[0]), y10[:], ACT.Copy)
        nc.vector.tensor_copy(listed(map1[:], halves[1]), y11[:])
        nc.sync.dma_start(out[0, P:NQ, :], map1[:])
